import numpy as np
import ml_dtypes


def mxq(x, axis, fmt="e4m3"):
    dtype, down = {"e4m3": (ml_dtypes.float8_e4m3fn, 7), "e5m2": (ml_dtypes.float8_e5m2, 14)}[fmt]
    v = np.moveaxis(np.asarray(x, np.float32).astype(ml_dtypes.bfloat16).astype(np.float64), axis, -1)
    blocks = v.reshape(v.shape[:-1] + (-1, 32))
    amax = np.abs(blocks).max(-1, keepdims=True)
    byte = np.maximum(np.where(amax > 0, np.frexp(amax)[1] - 1 + 127, 0) - down, 1)
    scale = np.exp2(byte - 127.0)
    codes = (blocks / scale).astype(np.float32).astype(dtype).astype(np.float64)
    return np.moveaxis((codes * scale).reshape(v.shape), -1, axis)


WIDE = False


def mx_kscale(k):
    if not WIDE:
        return np.ones(k)
    levels = np.array([10, -10, 5, -5, 0])
    if k % 512:
        return np.exp2(np.random.permutation(np.resize(levels, k // 32))).repeat(32)
    a = np.empty((k // 512, 16))
    for p in range(k // 512):
        a[p, :8] = np.random.permutation(np.resize(levels, 8))
        for g in range(8):
            far = levels[np.abs(levels - a[p, g]) >= 10]
            a[p, g + 8] = far[np.random.randint(len(far))]
    return np.exp2(a.ravel()).repeat(32)


def f64(x):
    return np.asarray(x).astype(np.float64)


def striped(idx):
    return np.tile(idx.reshape(-1, 16).T, (8, 1)).astype(np.uint16)


def unstriped(offs):
    return offs[:16].T.reshape(-1).astype(np.int64)


E2M1 = np.array([0.0, 0.5, 1.0, 1.5, 2.0, 3.0, 4.0, 6.0, -0.0, -0.5, -1.0, -1.5, -2.0, -3.0, -4.0, -6.0])


def pack_weight(w, fmt):
    k, n = w.shape
    w = f64(np.asarray(w, np.float32).astype(ml_dtypes.bfloat16)).reshape(k // 32, 32, n)
    amax = np.abs(w).max(1)
    if fmt == "e4m3":
        byte = np.frexp(amax)[1] - 1 + 127 - 7
    else:
        mant, ex = np.frexp(amax / 6.0)
        byte = np.where(mant > 0.5, ex, ex - 1) + 127
    byte = np.clip(np.where(amax > 0, byte, 1), 1, 254)
    scaled = (w * np.exp2(127.0 - byte)[:, None, :]).reshape(k, n).astype(np.float32)
    by_word = np.ascontiguousarray(scaled.reshape(k // 512, 128, 4, n).transpose(0, 1, 3, 2))
    if fmt == "e4m3":
        words = by_word.astype(ml_dtypes.float8_e4m3fn).view(np.uint8)
    else:
        c = by_word.astype(ml_dtypes.float4_e2m1fn).view(np.uint8) & 0xF
        words = (c[..., 0::2] | (c[..., 1::2] << 4)).reshape(k // 512, 128, 2 * n)
    return np.ascontiguousarray(words), np.ascontiguousarray(byte.astype(np.uint8).reshape(k // 512, 16, n))


def unpack_weight(words, scales, fmt):
    g, _, n = scales.shape
    words = np.ascontiguousarray(words).reshape(g, 128, n, -1)
    if fmt == "e4m3":
        vals = words.view(ml_dtypes.float8_e4m3fn).astype(np.float64)
    else:
        nib = np.empty((g, 128, n, 4), np.uint8)
        nib[..., 0::2] = words & 0xF
        nib[..., 1::2] = words >> 4
        vals = E2M1[nib]
    vals = vals * np.repeat(np.exp2(scales.astype(np.float64) - 127.0), 8, axis=1)[..., None]
    return vals.transpose(0, 1, 3, 2).reshape(g * 512, n)


def gelu(v):
    return 0.5 * v * (1.0 + np.tanh(np.sqrt(2.0 / np.pi) * (v + 0.044715 * v**3)))


K, T, E, C, N = 1536, 640, 20, 128, 128
TOP = 4
K8 = 512


def by_expert(wq, xq):
    return np.concatenate([wq[e].T @ xq[:, e * C:(e + 1) * C] for e in range(E)], axis=1)


def setup_inputs():
    n = np.random.standard_normal
    s = mx_kscale(K)[:, None]
    deal = np.repeat(np.arange(E), C).reshape(TOP, T)[:, np.random.permutation(T)]
    deal = np.take_along_axis(deal, np.argsort(np.random.rand(TOP, T), axis=0), axis=0)
    for _ in range(8):
        s_, t_ = np.random.permutation(T).reshape(2, -1); r = np.random.randint(TOP, size=T // 2); x, y = deal[r, s_].copy(), deal[r, t_].copy()
        ok = ~((deal[:, s_] == y).any(0) | (deal[:, t_] == x).any(0)); deal[r[ok], s_[ok]] = y[ok]; deal[r[ok], t_[ok]] = x[ok]
    order = np.lexsort((np.random.rand(TOP * T), deal.reshape(-1)))
    slot_token = order % T; pos = np.empty(TOP * T, np.int64); pos[order] = np.arange(TOP * T); pos = pos.reshape(TOP, T)
    g = np.random.uniform(0.5, 1.5, (TOP, T)); g = g / g.sum(0)
    w = n((E, K, N)) / np.sqrt(K) / s[None]
    w8 = [pack_weight(m[:K8], "e4m3") for m in w]
    w4 = [pack_weight(m[K8:], "e2m1") for m in w]
    return {
        "xT": (n((K, T)) * s).astype(np.float32),
        "w8_words": np.stack([m[0] for m in w8]),
        "w8_scales": np.stack([m[1] for m in w8]),
        "w4_words": np.stack([m[0] for m in w4]),
        "w4_scales": np.stack([m[1] for m in w4]),
        "b": (0.3 * n((N, E))).astype(np.float32),
        "gate": np.stack([np.tile(r, (N, 1)) for r in g]).astype(np.float32),
        "offs": striped(slot_token),
        "pos1": striped(pos[0]),
        "pos2": striped(pos[1]),
        "pos3": striped(pos[2]),
        "pos4": striped(pos[3]),
    }


def reference(xT, w8_words, w8_scales, w4_words, w4_scales, b, gate, offs, pos1, pos2, pos3, pos4):
    idx = unstriped(offs)
    w = np.stack([np.concatenate([unpack_weight(w8_words[e], w8_scales[e], "e4m3"), unpack_weight(w4_words[e], w4_scales[e], "e2m1")]) for e in range(E)])
    xq = mxq(f64(xT)[:, idx], 0, "e4m3")
    y = by_expert(w, xq)
    y = gelu(y + np.repeat(f64(b), C, axis=1))
    return sum(f64(gate[r]) * y[:, unstriped(p)] for r, p in enumerate((pos1, pos2, pos3, pos4)))

@@ -1,0 +1,228 @@
+from contextlib import ExitStack
+
+import concourse.mybir as mybir
+
+F32 = mybir.dt.float32
+BF16 = mybir.dt.bfloat16
+I32 = mybir.dt.int32
+U32 = mybir.dt.uint32
+U16 = mybir.dt.uint16
+U8 = mybir.dt.uint8
+FP8X4 = mybir.dt.float8_e4m3fn_x4
+FP4X4 = mybir.dt.float4_e2m1fn_x4
+MULT = mybir.AluOpType.mult
+ADD = mybir.AluOpType.add
+GELU = mybir.ActivationFunctionType.Gelu_apprx_tanh
+
+P = 128
+K, T, E, C, N, TOP = 1536, 640, 20, 128, 128, 4
+PASSES = 3
+S = E * C
+FLOPS = 2 * S * K * N
+
+WIN = 1728
+HALF = S // 2
+WIN2 = 704
+PLANE = (4, 0, 8)
+
+
+def tile_moe_tk_lin_gelu_kernel(
+    tc, xT, w8_words, w8_scales, w4_words, w4_scales, b, gate, offs, pos1, pos2, pos3, pos4, out
+):
+    nc = tc.nc
+    with ExitStack() as ctx:
+        lists = ctx.enter_context(tc.tile_pool(name="lists", bufs=1))
+        keep = ctx.enter_context(tc.tile_pool(name="keep", bufs=1))
+        late = ctx.enter_context(tc.tile_pool(name="late", bufs=1))
+        hold = ctx.enter_context(tc.tile_pool(name="hold", bufs=1))
+        psum = ctx.enter_context(tc.psum_pool(name="psum", bufs=8))
+
+        offs_sb = lists.tile([P, S // 16], U16, name="offs_sb")
+        pos_sb = [lists.tile([P, T // 16], U16, name=f"pos{r}_sb") for r in range(TOP)]
+
+        def x_rows(a):
+            return xT[512 * a : 512 * (a + 1), :].rearrange("(p j) t -> p j t", j=4)
+
+        x0a = keep.tile([P, 4, 512], F32, name="x0a")
+        x0b = keep.tile([P, 4, 128], F32, name="x0b")
+        x1 = keep.tile([P, 4, T], F32, name="x1")
+        x2 = keep.tile([P, 4, T], F32, name="x2")
+        nc.sync.dma_start(out=x0a[:], in_=x_rows(0)[:, :, 0:512])
+        nc.sync.dma_start(out=x0b[:], in_=x_rows(0)[:, :, 512:640])
+        nc.sync.dma_start(offs_sb[:], offs)
+        nc.sync.dma_start(out=x1[:], in_=x_rows(1))
+        nc.sync.dma_start(out=x2[:], in_=x_rows(2))
+
+        tiny = keep.tile([P, 8], F32, name="tiny")
+        tiny2 = keep.tile([P, 8], F32, name="tiny2")
+        nc.gpsimd.memset(tiny[:], 0.0)
+        nc.scalar.activation(out=tiny2[:], in_=tiny[:], func=GELU)
+        codes = [keep.tile([P, WIN if a < 1 else WIN2], I32, name=f"codes{a}", align_bytes=64) for a in range(PASSES)]
+        bytes_i32 = late.tile([P, WIN // 4], I32, name="bytes_i32", tag="late", align_bytes=64)
+        bytes_all = bytes_i32[:].bitcast(U8)
+        nc.vector.memset(bytes_i32[:], 0)
+        for a in range(PASSES):
+            nc.vector.memset(codes[a][:, T:], 0)
+        w_s = keep.tile([P, 3 * E * N // 4], I32, name="w_s", align_bytes=64)
+        g_moved = keep.tile([P, S // 4], I32, name="g_moved", align_bytes=64)
+        nc.gpsimd.memset(w_s[:], 0)
+        nc.gpsimd.memset(g_moved[:], 0)
+
+        stage = keep.tile([16, 3 * E, N // 4], I32, name="stage")
+        nc.sync.dma_start(out=stage[:, 0:E, :], in_=w8_scales.bitcast(I32).rearrange("e a q n -> q (e a) n"))
+        nc.sync.dma_start(out=stage[:, E:, :], in_=w4_scales.bitcast(I32).rearrange("e a q n -> q (e a) n"))
+        EH = E // 2
+        w8 = [keep.tile([P, EH, N], I32, name=f"w8_{h}", align_bytes=64) for h in range(2)]
+        w4 = [keep.tile([P, EH, 2, N // 2], I32, name=f"w4_{h}", align_bytes=64) for h in range(2)]
+        b_sb = keep.tile([P, E], F32, name="b_sb")
+
+        def load_w8(h):
+            nc.sync.dma_start(
+                out=w8[h][:],
+                in_=w8_words[h * EH : (h + 1) * EH].rearrange("e a p n r -> p (e a) (n r)").bitcast(I32),
+            )
+
+        def load_w4(h):
+            nc.sync.dma_start(
+                out=w4[h][:].rearrange("p e a n -> p (e a) n"),
+                in_=w4_words[h * EH : (h + 1) * EH].rearrange("e a p n -> p (e a) n").bitcast(I32),
+            )
+
+        load_w8(0)
+        for q in range(4):
+            nc.sync.dma_start(
+                out=w_s[32 * q : 32 * q + 4, :], in_=stage[4 * q : 4 * q + 4, :, :].rearrange("p g n -> p (g n)")
+            )
+        load_w4(0)
+        nc.sync.dma_start(out=b_sb[:], in_=b)
+        load_w8(1)
+        load_w4(1)
+        for r, pos in enumerate((pos1, pos2, pos3, pos4)):
+            nc.sync.dma_start(pos_sb[r][:], pos)
+
+        xb = [keep.tile([P, T, 4], BF16, name=f"xb{a}", align_bytes=64) for a in range(2)]
+        xb.append(hold.tile([P, T, 4], BF16, name="xb2", tag="hold", align_bytes=64))
+
+        def lay(copy, a, src, c0, c1, s0):
+            copy(
+                out=xb[a][:, c0:c1, :].rearrange("p (c i) j -> p c j i", i=4),
+                in_=src[:, :, c0 - s0 : c1 - s0].rearrange("p j (c i) -> p c j i", i=4),
+            )
+
+        def quantise(a, c0, c1):
+            k = PLANE[a]
+            nc.vector.quantize_mx(
+                out=codes[a][:, c0:c1].bitcast(FP8X4),
+                scales=bytes_all[k:P, c0:c1],
+                in_=xb[a][:, c0:c1, :].rearrange("p n j -> p (n j)"),
+            )
+
+        words = {(a, 0): keep.tile([P, S], U32, name=f"words{a}", align_bytes=64) for a in (0, 2)}
+        words[1, 0] = keep.tile([P, 8 * C], U32, name="words1a", align_bytes=64)
+        g_bytes = keep.tile([P, S], U8, name="g_bytes", align_bytes=64)
+
+        def word_cols(a, s0, s1):
+            if a == 1 and s0 >= 8 * C:
+                return words[1, 1][:, s0 - 8 * C : s1 - 8 * C]
+            return words[a, 0][:, s0:s1]
+
+        def gather_words(a, s0, s1):
+            nc.vector.tensor_copy(
+                out=word_cols(a, s0, s1), in_=codes[a][:].bitcast(U32).indirect(offs_sb[:, s0 // 16 : s1 // 16])
+            )
+
+        def gather_bytes(s0, s1):
+            nc.vector.tensor_copy(out=g_bytes[:, s0:s1], in_=bytes_all.indirect(offs_sb[:, s0 // 16 : s1 // 16]))
+            nc.scalar.dma_start(out=g_moved[0 : P - 8, s0 // 4 : s1 // 4], in_=g_bytes[8:P, s0:s1].bitcast(I32))
+
+        lay(nc.vector.tensor_copy, 0, x0a, 0, 384, 0)
+        lay(nc.scalar.copy, 0, x0a, 384, 512, 0)
+        lay(nc.scalar.copy, 0, x0b, 512, 640, 512)
+        quantise(0, 0, 512)
+        quantise(0, 512, 640)
+        lay(nc.scalar.copy, 1, x1, 0, 640, 0)
+        lay(nc.scalar.copy, 2, x2, 0, 640, 0)
+        gather_words(0, 0, HALF)
+        gather_words(0, HALF, S)
+        quantise(1, 0, 512)
+        quantise(1, 512, 640)
+        gather_words(1, 0, 4 * C)
+        gather_words(1, 4 * C, 8 * C)
+        quantise(2, 0, 512)
+        quantise(2, 512, 640)
+        words[1, 1] = hold.tile([P, S - 8 * C], U32, name="words1b", tag="hold", align_bytes=64)
+
+        y = keep.tile([P, S], F32, name="y")
+        moved8 = g_moved[:].bitcast(U8)
+        w_s8 = w_s[:].bitcast(U8)
+
+        def multiply(e, acc, passes):
+            h, el = divmod(e, EH)
+            cols = slice(e * C, (e + 1) * C)
+            for a in passes:
+                if a == 0:
+                    lhs, lhs_scale, plane = w8[h][:, el, :].bitcast(FP8X4), w_s8[:, e * N : (e + 1) * N], g_bytes[4:P, cols]
+                else:
+                    g = E + 2 * e + a - 1
+                    lhs, lhs_scale = w4[h][:, el, a - 1, :].bitcast(FP4X4), w_s8[:, g * N : (g + 1) * N]
+                    plane = g_bytes[:, cols] if a == 1 else moved8[:, cols]
+                nc.tensor.matmul_mx(
+                    out=acc, lhsT=lhs, lhsT_scale=lhs_scale, rhs=word_cols(a, e * C, (e + 1) * C).bitcast(FP8X4), rhs_scale=plane,
+                    start=(a == 0), stop=(a == 2),
+                )
+
+        def activate(e, acc):
+            nc.scalar.activation(out=y[:, e * C : (e + 1) * C], in_=acc, func=GELU, bias=b_sb[:, e : e + 1])
+
+        accs = {}
+
+        def first_two(e0):
+            if e0 >= 8:
+                gather_words(1, e0 * C, (e0 + 4) * C)
+            for e in range(e0, e0 + 4):
+                accs[e] = psum.tile([P, C], F32, name="acc")
+                multiply(e, accs[e][:], (0, 1))
+
+        def third(e0, e1):
+            gather_words(2, e0 * C, e1 * C)
+            for e in range(e0, e1):
+                multiply(e, accs[e][:], (2,))
+                activate(e, accs[e][:])
+
+        gather_bytes(0, HALF)
+        first_two(0)
+        first_two(4)
+        gather_bytes(HALF, S)
+        gate_sb = late.tile([P, TOP, T], F32, name="gate_sb", tag="late", align_bytes=64)
+        nc.sync.dma_start(out=gate_sb[:], in_=gate.rearrange("r p t -> p r t"))
+        third(0, 4)
+        third(4, 8)
+        first_two(8)
+        third(8, 12)
+        first_two(12)
+        third(12, 16)
+        first_two(16)
+        third(16, 19)
+        third(19, 20)
+
+        prod = [keep.tile([P, T], F32, name=f"prod{r}") for r in range(TOP)]
+        s01 = keep.tile([P, T], F32, name="s01")
+        s23 = keep.tile([P, T], F32, name="s23")
+        res = keep.tile([P, T], F32, name="res")
+
+        def fetch(r):
+            nc.vector.tensor_tensor(prod[r][:], y[:].indirect(pos_sb[r][:]), gate_sb[:, r, :], MULT)
+
+        fetch(0)
+        fetch(1)
+        fetch(2)
+        nc.vector.tensor_tensor(s01[:], prod[0][:], prod[1][:], ADD)
+        fetch(3)
+        TH = T // 2
+        for t0 in (0, TH):
+            cols = slice(t0, t0 + TH)
+            nc.vector.tensor_tensor(s23[:, cols], s01[:, cols], prod[2][:, cols], ADD)
+        for t0 in (0, TH):
+            cols = slice(t0, t0 + TH)
+            nc.vector.tensor_tensor(res[:, cols], s23[:, cols], prod[3][:, cols], ADD)
+            nc.sync.dma_start(out=out[:, cols], in_=res[:, cols])

@@ -1,6 +1,7 @@
 from contextlib import ExitStack
 
 import concourse.mybir as mybir
+from concourse.masks import make_identity
 
 F32 = mybir.dt.float32
 BF16 = mybir.dt.bfloat16
@@ -43,12 +44,14 @@ def tile_moe_tk_lin_gelu_kernel(
         def x_rows(a):
             return xT[512 * a : 512 * (a + 1), :].rearrange("(p j) t -> p j t", j=4)
 
-        x0a = keep.tile([P, 4, 512], F32, name="x0a")
-        x0b = keep.tile([P, 4, 128], F32, name="x0b")
+        x0a = keep.tile([P, 4, 256], F32, name="x0a")
+        x0b = keep.tile([P, 4, 256], F32, name="x0b")
+        x0c = keep.tile([P, 4, 128], F32, name="x0c")
         x1 = keep.tile([P, 4, T], F32, name="x1")
         x2 = keep.tile([P, 4, T], F32, name="x2")
-        nc.sync.dma_start(out=x0a[:], in_=x_rows(0)[:, :, 0:512])
-        nc.sync.dma_start(out=x0b[:], in_=x_rows(0)[:, :, 512:640])
+        nc.sync.dma_start(out=x0a[:], in_=x_rows(0)[:, :, 0:256])
+        nc.sync.dma_start(out=x0b[:], in_=x_rows(0)[:, :, 256:512])
+        nc.sync.dma_start(out=x0c[:], in_=x_rows(0)[:, :, 512:640])
         nc.sync.dma_start(offs_sb[:], offs)
         nc.sync.dma_start(out=x1[:], in_=x_rows(1))
         nc.sync.dma_start(out=x2[:], in_=x_rows(2))
@@ -67,6 +70,8 @@ def tile_moe_tk_lin_gelu_kernel(
         g_moved = keep.tile([P, S // 4], I32, name="g_moved", align_bytes=64)
         nc.gpsimd.memset(w_s[:], 0)
         nc.gpsimd.memset(g_moved[:], 0)
+        ident = keep.tile([P, P], F32, name="ident")
+        make_identity(nc, ident[:])
 
         stage = keep.tile([16, 3 * E, N // 4], I32, name="stage")
         nc.sync.dma_start(out=stage[:, 0:E, :], in_=w8_scales.bitcast(I32).rearrange("e a q n -> q (e a) n"))
@@ -135,10 +140,14 @@ def tile_moe_tk_lin_gelu_kernel(
             nc.vector.tensor_copy(out=g_bytes[:, s0:s1], in_=bytes_all.indirect(offs_sb[:, s0 // 16 : s1 // 16]))
             nc.scalar.dma_start(out=g_moved[0 : P - 8, s0 // 4 : s1 // 4], in_=g_bytes[8:P, s0:s1].bitcast(I32))
 
-        lay(nc.vector.tensor_copy, 0, x0a, 0, 384, 0)
-        lay(nc.scalar.copy, 0, x0a, 384, 512, 0)
-        lay(nc.scalar.copy, 0, x0b, 512, 640, 512)
-        quantise(0, 0, 512)
+        lay(nc.vector.tensor_copy, 0, x0a, 0, 192, 0)
+        lay(nc.scalar.copy, 0, x0a, 192, 256, 0)
+        quantise(0, 0, 256)
+        lay(nc.vector.tensor_copy, 0, x0b, 256, 416, 256)
+        lay(nc.scalar.copy, 0, x0b, 416, 512, 256)
+        lay(nc.vector.tensor_copy, 0, x0c, 512, 608, 512)
+        lay(nc.scalar.copy, 0, x0c, 608, 640, 512)
+        quantise(0, 256, 512)
         quantise(0, 512, 640)
         lay(nc.scalar.copy, 1, x1, 0, 640, 0)
         lay(nc.scalar.copy, 2, x2, 0, 640, 0)
@@ -196,33 +205,52 @@ def tile_moe_tk_lin_gelu_kernel(
         gate_sb = late.tile([P, TOP, T], F32, name="gate_sb", tag="late", align_bytes=64)
         nc.sync.dma_start(out=gate_sb[:], in_=gate.rearrange("r p t -> p r t"))
         third(0, 4)
-        third(4, 8)
         first_two(8)
-        third(8, 12)
+        third(4, 8)
         first_two(12)
-        third(12, 16)
+        third(8, 12)
         first_two(16)
-        third(16, 19)
+        third(12, 16)
+        third(16, 18)
+        third(18, 19)
         third(19, 20)
 
-        prod = [keep.tile([P, T], F32, name=f"prod{r}") for r in range(TOP)]
-        s01 = keep.tile([P, T], F32, name="s01")
-        s23 = keep.tile([P, T], F32, name="s23")
-        res = keep.tile([P, T], F32, name="res")
+        halves = ((0, 3), (3, 5))
+        prod = [[keep.tile([P, (c1 - c0) * P], F32, name=f"prod{r}_{c0}") for c0, c1 in halves] for r in range(TOP)]
+        res = [keep.tile([P, (c1 - c0) * P], F32, name=f"res{c0}") for c0, c1 in halves]
+        turned = [keep.tile([P, P], F32, name=f"turned{c}") for c in range(T // P)]
+        sums = [psum.tile([P, P], F32, name="acc") for c in range(T // P)]
 
-        def fetch(r):
-            nc.vector.tensor_tensor(prod[r][:], y[:].indirect(pos_sb[r][:]), gate_sb[:, r, :], MULT)
+        def fetch(r, h):
+            c0, c1 = halves[h]
+            nc.vector.tensor_tensor(
+                prod[r][h][:], y[:].indirect(pos_sb[r][:, c0 * 8 : c1 * 8]), gate_sb[:, r, c0 * P : c1 * P], MULT
+            )
+            if r < TOP - 1:
+                for c in range(c0, c1):
+                    nc.tensor.matmul(
+                        sums[c][:], prod[r][h][:, (c - c0) * P : (c - c0 + 1) * P], ident[:],
+                        start=(r == 0), stop=(r == TOP - 2), is_transpose=True,
+                    )
 
-        fetch(0)
-        fetch(1)
-        fetch(2)
-        nc.vector.tensor_tensor(s01[:], prod[0][:], prod[1][:], ADD)
-        fetch(3)
-        TH = T // 2
-        for t0 in (0, TH):
-            cols = slice(t0, t0 + TH)
-            nc.vector.tensor_tensor(s23[:, cols], s01[:, cols], prod[2][:, cols], ADD)
-        for t0 in (0, TH):
-            cols = slice(t0, t0 + TH)
-            nc.vector.tensor_tensor(res[:, cols], s23[:, cols], prod[3][:, cols], ADD)
-            nc.sync.dma_start(out=out[:, cols], in_=res[:, cols])
+        back = {}
+
+        def turn_back(h):
+            c0, c1 = halves[h]
+            back[h] = psum.tile([P, (c1 - c0) * P], F32, name="acc")
+            for c in range(c0, c1):
+                nc.scalar.copy(out=turned[c][:], in_=sums[c][:])
+                nc.tensor.transpose(back[h][:, (c - c0) * P : (c - c0 + 1) * P], turned[c][:], ident[:])
+
+        def finish(h):
+            c0, c1 = halves[h]
+            nc.vector.tensor_tensor(res[h][:], prod[TOP - 1][h][:], back[h][:], ADD)
+            nc.sync.dma_start(out=out[:, c0 * P : c1 * P], in_=res[h][:])
+
+        for h in range(2):
+            for r in range(TOP - 1):
+                fetch(r, h)
+            turn_back(h)
+        for h in range(2):
+            fetch(TOP - 1, h)
+            finish(h)

@@ -21,9 +21,10 @@ PASSES = 3
 S = E * C
 FLOPS = 2 * S * K * N
 
-WIN = 1728
-HALF = S // 2
-WIN2 = 704
+WINS = (1408, 704, 704)
+WIN_BYTES = 2048
+NB = T // P
+G = 4 * C
 PLANE = (4, 0, 8)
 
 
@@ -34,7 +35,6 @@ def tile_moe_tk_lin_gelu_kernel(
     with ExitStack() as ctx:
         lists = ctx.enter_context(tc.tile_pool(name="lists", bufs=1))
         keep = ctx.enter_context(tc.tile_pool(name="keep", bufs=1))
-        late = ctx.enter_context(tc.tile_pool(name="late", bufs=1))
         hold = ctx.enter_context(tc.tile_pool(name="hold", bufs=1))
         psum = ctx.enter_context(tc.psum_pool(name="psum", bufs=8))
 
@@ -47,31 +47,41 @@ def tile_moe_tk_lin_gelu_kernel(
         x0a = keep.tile([P, 4, 256], F32, name="x0a")
         x0b = keep.tile([P, 4, 256], F32, name="x0b")
         x0c = keep.tile([P, 4, 128], F32, name="x0c")
-        x1 = keep.tile([P, 4, T], F32, name="x1")
-        x2 = keep.tile([P, 4, T], F32, name="x2")
+        x1a = keep.tile([P, 4, T // 2], F32, name="x1a")
+        x1b = hold.tile([P, 4, T // 2], F32, name="x1b", tag="hold1", align_bytes=64)
+        x2a = keep.tile([P, 4, T // 2], F32, name="x2a")
+        x2b = hold.tile([P, 4, T // 2], F32, name="x2b", tag="hold2", align_bytes=64)
         nc.sync.dma_start(out=x0a[:], in_=x_rows(0)[:, :, 0:256])
         nc.sync.dma_start(out=x0b[:], in_=x_rows(0)[:, :, 256:512])
         nc.sync.dma_start(out=x0c[:], in_=x_rows(0)[:, :, 512:640])
         nc.sync.dma_start(offs_sb[:], offs)
-        nc.sync.dma_start(out=x1[:], in_=x_rows(1))
-        nc.sync.dma_start(out=x2[:], in_=x_rows(2))
+        nc.sync.dma_start(out=x1a[:], in_=x_rows(1)[:, :, 0 : T // 2])
+        nc.sync.dma_start(out=x1b[:], in_=x_rows(1)[:, :, T // 2 : T])
+        nc.sync.dma_start(out=x2a[:], in_=x_rows(2)[:, :, 0 : T // 2])
+        nc.sync.dma_start(out=x2b[:], in_=x_rows(2)[:, :, T // 2 : T])
 
         tiny = keep.tile([P, 8], F32, name="tiny")
         tiny2 = keep.tile([P, 8], F32, name="tiny2")
         nc.gpsimd.memset(tiny[:], 0.0)
         nc.scalar.activation(out=tiny2[:], in_=tiny[:], func=GELU)
-        codes = [keep.tile([P, WIN if a < 1 else WIN2], I32, name=f"codes{a}", align_bytes=64) for a in range(PASSES)]
-        bytes_i32 = late.tile([P, WIN // 4], I32, name="bytes_i32", tag="late", align_bytes=64)
+        codes = [keep.tile([P, WINS[a]], I32, name=f"codes{a}", align_bytes=64) for a in range(PASSES)]
+        bytes_i32 = keep.tile([P, WIN_BYTES // 4], I32, name="bytes_i32", align_bytes=64)
         bytes_all = bytes_i32[:].bitcast(U8)
         nc.vector.memset(bytes_i32[:], 0)
         for a in range(PASSES):
             nc.vector.memset(codes[a][:, T:], 0)
         w_s = keep.tile([P, 3 * E * N // 4], I32, name="w_s", align_bytes=64)
         g_moved = keep.tile([P, S // 4], I32, name="g_moved", align_bytes=64)
-        nc.gpsimd.memset(w_s[:], 0)
+        nc.vector.memset(w_s[:], 0)
         nc.gpsimd.memset(g_moved[:], 0)
         ident = keep.tile([P, P], F32, name="ident")
         make_identity(nc, ident[:])
+        gate_rows = keep.tile([P, T], F32, name="gate_rows")
+        nc.gpsimd.memset(gate_rows[:], 0.0)
+
+        nc.sync.dma_start(out=gate_rows[0:TOP, :], in_=gate[:, 0, :])
+        b_sb = keep.tile([P, E], F32, name="b_sb")
+        nc.sync.dma_start(out=b_sb[:], in_=b)
 
         stage = keep.tile([16, 3 * E, N // 4], I32, name="stage")
         nc.sync.dma_start(out=stage[:, 0:E, :], in_=w8_scales.bitcast(I32).rearrange("e a q n -> q (e a) n"))
@@ -79,7 +89,6 @@ def tile_moe_tk_lin_gelu_kernel(
         EH = E // 2
         w8 = [keep.tile([P, EH, N], I32, name=f"w8_{h}", align_bytes=64) for h in range(2)]
         w4 = [keep.tile([P, EH, 2, N // 2], I32, name=f"w4_{h}", align_bytes=64) for h in range(2)]
-        b_sb = keep.tile([P, E], F32, name="b_sb")
 
         def load_w8(h):
             nc.sync.dma_start(
@@ -94,19 +103,18 @@ def tile_moe_tk_lin_gelu_kernel(
             )
 
         load_w8(0)
+        load_w4(0)
         for q in range(4):
             nc.sync.dma_start(
                 out=w_s[32 * q : 32 * q + 4, :], in_=stage[4 * q : 4 * q + 4, :, :].rearrange("p g n -> p (g n)")
             )
-        load_w4(0)
-        nc.sync.dma_start(out=b_sb[:], in_=b)
         load_w8(1)
         load_w4(1)
         for r, pos in enumerate((pos1, pos2, pos3, pos4)):
             nc.sync.dma_start(pos_sb[r][:], pos)
 
         xb = [keep.tile([P, T, 4], BF16, name=f"xb{a}", align_bytes=64) for a in range(2)]
-        xb.append(hold.tile([P, T, 4], BF16, name="xb2", tag="hold", align_bytes=64))
+        xb.append(hold.tile([P, T, 4], BF16, name="xb2", tag="hold3", align_bytes=64))
 
         def lay(copy, a, src, c0, c1, s0):
             copy(
@@ -122,14 +130,14 @@ def tile_moe_tk_lin_gelu_kernel(
                 in_=xb[a][:, c0:c1, :].rearrange("p n j -> p (n j)"),
             )
 
-        words = {(a, 0): keep.tile([P, S], U32, name=f"words{a}", align_bytes=64) for a in (0, 2)}
-        words[1, 0] = keep.tile([P, 8 * C], U32, name="words1a", align_bytes=64)
+        words = {a: [] for a in range(PASSES)}
         g_bytes = keep.tile([P, S], U8, name="g_bytes", align_bytes=64)
 
+        def word_tile(a, s0, s1, pool, tag):
+            words[a].append((s0, s1, pool.tile([P, s1 - s0], U32, name=f"words{a}_{s0}", tag=tag, align_bytes=64)))
+
         def word_cols(a, s0, s1):
-            if a == 1 and s0 >= 8 * C:
-                return words[1, 1][:, s0 - 8 * C : s1 - 8 * C]
-            return words[a, 0][:, s0:s1]
+            return [t[:, s0 - t0 : s1 - t0] for t0, t1, t in words[a] if t0 <= s0 and s1 <= t1][0]
 
         def gather_words(a, s0, s1):
             nc.vector.tensor_copy(
@@ -138,7 +146,9 @@ def tile_moe_tk_lin_gelu_kernel(
 
         def gather_bytes(s0, s1):
             nc.vector.tensor_copy(out=g_bytes[:, s0:s1], in_=bytes_all.indirect(offs_sb[:, s0 // 16 : s1 // 16]))
-            nc.scalar.dma_start(out=g_moved[0 : P - 8, s0 // 4 : s1 // 4], in_=g_bytes[8:P, s0:s1].bitcast(I32))
+
+        def move_plane(s0, s1):
+            nc.sync.dma_start(out=g_moved[0 : P - 8, s0 // 4 : s1 // 4], in_=g_bytes[8:P, s0:s1].bitcast(I32))
 
         lay(nc.vector.tensor_copy, 0, x0a, 0, 192, 0)
         lay(nc.scalar.copy, 0, x0a, 192, 256, 0)
@@ -149,17 +159,42 @@ def tile_moe_tk_lin_gelu_kernel(
         lay(nc.scalar.copy, 0, x0c, 608, 640, 512)
         quantise(0, 256, 512)
         quantise(0, 512, 640)
-        lay(nc.scalar.copy, 1, x1, 0, 640, 0)
-        lay(nc.scalar.copy, 2, x2, 0, 640, 0)
-        gather_words(0, 0, HALF)
-        gather_words(0, HALF, S)
+        lay(nc.scalar.copy, 1, x1a, 0, T // 2, 0)
+        lay(nc.scalar.copy, 1, x1b, T // 2, T, T // 2)
+        lay(nc.scalar.copy, 2, x2a, 0, T // 2, 0)
+        lay(nc.scalar.copy, 2, x2b, T // 2, T, T // 2)
+        word_tile(0, 0, 4 * G, keep, "w0a")
+        word_tile(1, 0, G, keep, "w1a")
+        word_tile(2, 0, S, keep, "w2")
+        gather_words(0, 0, 2 * G)
+        gather_words(0, 2 * G, 4 * G)
         quantise(1, 0, 512)
         quantise(1, 512, 640)
-        gather_words(1, 0, 4 * C)
-        gather_words(1, 4 * C, 8 * C)
+        word_tile(0, 4 * G, S, hold, "hold1")
+        gather_words(0, 4 * G, S)
+        gather_words(1, 0, G)
         quantise(2, 0, 512)
         quantise(2, 512, 640)
-        words[1, 1] = hold.tile([P, S - 8 * C], U32, name="words1b", tag="hold", align_bytes=64)
+        word_tile(1, G, 2 * G, hold, "hold2")
+        gather_words(1, G, 2 * G)
+        word_tile(1, 2 * G, S, hold, "hold3")
+
+        gate_cols = keep.tile([P, NB, TOP], F32, name="gate_cols")
+        for c0, c1 in ((0, 4), (4, NB)):
+            bank = psum.tile([P, c1 - c0, P], F32, name="acc")
+            for c in range(c0, c1):
+                nc.tensor.transpose(bank[:, c - c0, :], gate_rows[:, c * P : (c + 1) * P], ident[:])
+            nc.scalar.copy(out=gate_cols[:, c0:c1, :], in_=bank[:, :, 0:TOP])
+        gate_sb = keep.tile([P, TOP, T], F32, name="gate_sb")
+        gate_flat = gate_sb[:].rearrange("p r t -> p (r t)")
+        for j0 in range(0, TOP * NB, 4):
+            bank = psum.tile([P, 4 * P], F32, name="acc")
+            for j in range(j0, j0 + 4):
+                r, c = divmod(j, NB)
+                nc.tensor.transpose(
+                    bank[:, (j - j0) * P : (j - j0 + 1) * P], gate_cols[:, c, r : r + 1].to_broadcast([P, P]), ident[:]
+                )
+            nc.scalar.copy(out=gate_flat[:, j0 * P : (j0 + 4) * P], in_=bank[:])
 
         y = keep.tile([P, S], F32, name="y")
         moved8 = g_moved[:].bitcast(U8)
@@ -198,12 +233,12 @@ def tile_moe_tk_lin_gelu_kernel(
                 multiply(e, accs[e][:], (2,))
                 activate(e, accs[e][:])
 
-        gather_bytes(0, HALF)
+        gather_bytes(0, 2 * G)
+        move_plane(0, 2 * G)
         first_two(0)
         first_two(4)
-        gather_bytes(HALF, S)
-        gate_sb = late.tile([P, TOP, T], F32, name="gate_sb", tag="late", align_bytes=64)
-        nc.sync.dma_start(out=gate_sb[:], in_=gate.rearrange("r p t -> p r t"))
+        gather_bytes(2 * G, S)
+        move_plane(2 * G, S)
         third(0, 4)
         first_two(8)
         third(4, 8)
@@ -215,42 +250,41 @@ def tile_moe_tk_lin_gelu_kernel(
         third(18, 19)
         third(19, 20)
 
-        halves = ((0, 3), (3, 5))
-        prod = [[keep.tile([P, (c1 - c0) * P], F32, name=f"prod{r}_{c0}") for c0, c1 in halves] for r in range(TOP)]
-        res = [keep.tile([P, (c1 - c0) * P], F32, name=f"res{c0}") for c0, c1 in halves]
-        turned = [keep.tile([P, P], F32, name=f"turned{c}") for c in range(T // P)]
-        sums = [psum.tile([P, P], F32, name="acc") for c in range(T // P)]
+        halves = ((0, 3), (3, NB))
+        prod = [keep.tile([P, T], F32, name=f"prod{r}") for r in range(TOP)]
+        res = keep.tile([P, T], F32, name="res")
+        turned = [keep.tile([P, P], F32, name=f"turned{c}") for c in range(NB)]
+        sums = [psum.tile([P, P], F32, name="acc") for c in range(NB)]
 
-        def fetch(r, h):
-            c0, c1 = halves[h]
-            nc.vector.tensor_tensor(
-                prod[r][h][:], y[:].indirect(pos_sb[r][:, c0 * 8 : c1 * 8]), gate_sb[:, r, c0 * P : c1 * P], MULT
-            )
+        def fetch(r, c0, c1):
+            cols = slice(c0 * P, c1 * P)
+            nc.vector.tensor_tensor(prod[r][:, cols], y[:].indirect(pos_sb[r][:, c0 * 8 : c1 * 8]), gate_sb[:, r, cols], MULT)
             if r < TOP - 1:
                 for c in range(c0, c1):
                     nc.tensor.matmul(
-                        sums[c][:], prod[r][h][:, (c - c0) * P : (c - c0 + 1) * P], ident[:],
+                        sums[c][:], prod[r][:, c * P : (c + 1) * P], ident[:],
                         start=(r == 0), stop=(r == TOP - 2), is_transpose=True,
                     )
 
         back = {}
 
-        def turn_back(h):
-            c0, c1 = halves[h]
-            back[h] = psum.tile([P, (c1 - c0) * P], F32, name="acc")
+        def turn_back(c0, c1):
+            back[c0] = psum.tile([P, (c1 - c0) * P], F32, name="acc")
             for c in range(c0, c1):
                 nc.scalar.copy(out=turned[c][:], in_=sums[c][:])
-                nc.tensor.transpose(back[h][:, (c - c0) * P : (c - c0 + 1) * P], turned[c][:], ident[:])
+                nc.tensor.transpose(back[c0][:, (c - c0) * P : (c - c0 + 1) * P], turned[c][:], ident[:])
 
-        def finish(h):
-            c0, c1 = halves[h]
-            nc.vector.tensor_tensor(res[h][:], prod[TOP - 1][h][:], back[h][:], ADD)
-            nc.sync.dma_start(out=out[:, c0 * P : c1 * P], in_=res[h][:])
+        def finish(c0, c1):
+            cols = slice(c0 * P, c1 * P)
+            nc.vector.tensor_tensor(res[:, cols], prod[TOP - 1][:, cols], back[c0][:], ADD)
+            nc.sync.dma_start(out=out[:, cols], in_=res[:, cols])
 
-        for h in range(2):
-            for r in range(TOP - 1):
-                fetch(r, h)
-            turn_back(h)
-        for h in range(2):
-            fetch(TOP - 1, h)
-            finish(h)
+        fetch(0, 0, NB)
+        fetch(1, 0, NB)
+        for c0, c1 in halves:
+            fetch(2, c0, c1)
+            turn_back(c0, c1)
+        for c0, c1 in halves:
+            fetch(3, c0, c1)
+        for c0, c1 in halves:
+            finish(c0, c1)

@@ -21,7 +21,7 @@ PASSES = 3
 S = E * C
 FLOPS = 2 * S * K * N
 
-WINS = (1408, 704, 704)
+WINS = (1536, 704, 704)
 WIN_BYTES = 2048
 NB = T // P
 G = 4 * C
@@ -49,7 +49,7 @@ def tile_moe_tk_lin_gelu_kernel(
         x0c = keep.tile([P, 4, 128], F32, name="x0c")
         x1a = keep.tile([P, 4, T // 2], F32, name="x1a")
         x1b = hold.tile([P, 4, T // 2], F32, name="x1b", tag="hold1", align_bytes=64)
-        x2a = keep.tile([P, 4, T // 2], F32, name="x2a")
+        x2a = hold.tile([P, 4, T // 2], F32, name="x2a", tag="hold4", align_bytes=64)
         x2b = hold.tile([P, 4, T // 2], F32, name="x2b", tag="hold2", align_bytes=64)
         nc.sync.dma_start(out=x0a[:], in_=x_rows(0)[:, :, 0:256])
         nc.sync.dma_start(out=x0b[:], in_=x_rows(0)[:, :, 256:512])
@@ -80,38 +80,29 @@ def tile_moe_tk_lin_gelu_kernel(
         nc.gpsimd.memset(gate_rows[:], 0.0)
 
         nc.sync.dma_start(out=gate_rows[0:TOP, :], in_=gate[:, 0, :])
+
         b_sb = keep.tile([P, E], F32, name="b_sb")
         nc.sync.dma_start(out=b_sb[:], in_=b)
 
-        stage = keep.tile([16, 3 * E, N // 4], I32, name="stage")
-        nc.sync.dma_start(out=stage[:, 0:E, :], in_=w8_scales.bitcast(I32).rearrange("e a q n -> q (e a) n"))
-        nc.sync.dma_start(out=stage[:, E:, :], in_=w4_scales.bitcast(I32).rearrange("e a q n -> q (e a) n"))
-        EH = E // 2
-        w8 = [keep.tile([P, EH, N], I32, name=f"w8_{h}", align_bytes=64) for h in range(2)]
-        w4 = [keep.tile([P, EH, 2, N // 2], I32, name=f"w4_{h}", align_bytes=64) for h in range(2)]
+        stage = keep.tile([P, 3 * E, N // 4], I32, name="stage")
+        nc.sync.dma_start(out=stage[0:P:8, 0:E, :], in_=w8_scales.bitcast(I32).rearrange("e a q n -> q (e a) n"))
+        nc.sync.dma_start(out=stage[0:P:8, E:, :], in_=w4_scales.bitcast(I32).rearrange("e a q n -> q (e a) n"))
+        parts = ((0, 8), (8, 12), (12, 16), (16, E))
+        w8 = [keep.tile([P, e1 - e0, N], I32, name=f"w8_{e0}", align_bytes=64) for e0, e1 in parts]
+        w4 = [keep.tile([P, e1 - e0, 2, N // 2], I32, name=f"w4_{e0}", align_bytes=64) for e0, e1 in parts]
 
-        def load_w8(h):
-            nc.sync.dma_start(
-                out=w8[h][:],
-                in_=w8_words[h * EH : (h + 1) * EH].rearrange("e a p n r -> p (e a) (n r)").bitcast(I32),
-            )
-
-        def load_w4(h):
+        def load_weights(h):
+            e0, e1 = parts[h]
+            nc.sync.dma_start(out=w8[h][:], in_=w8_words[e0:e1].rearrange("e a p n r -> p (e a) (n r)").bitcast(I32))
             nc.sync.dma_start(
                 out=w4[h][:].rearrange("p e a n -> p (e a) n"),
-                in_=w4_words[h * EH : (h + 1) * EH].rearrange("e a p n -> p (e a) n").bitcast(I32),
+                in_=w4_words[e0:e1].rearrange("e a p n -> p (e a) n").bitcast(I32),
             )
 
-        load_w8(0)
-        load_w4(0)
-        for q in range(4):
-            nc.sync.dma_start(
-                out=w_s[32 * q : 32 * q + 4, :], in_=stage[4 * q : 4 * q + 4, :, :].rearrange("p g n -> p (g n)")
-            )
-        load_w8(1)
-        load_w4(1)
-        for r, pos in enumerate((pos1, pos2, pos3, pos4)):
-            nc.sync.dma_start(pos_sb[r][:], pos)
+        load_weights(0)
+        for r in range(4):
+            nc.sync.dma_start(out=w_s[r:P:32, :], in_=stage[8 * r : P : 32, :, :].rearrange("p g n -> p (g n)"))
+        load_weights(1)
 
         xb = [keep.tile([P, T, 4], BF16, name=f"xb{a}", align_bytes=64) for a in range(2)]
         xb.append(hold.tile([P, T, 4], BF16, name="xb2", tag="hold3", align_bytes=64))
@@ -163,23 +154,24 @@ def tile_moe_tk_lin_gelu_kernel(
         lay(nc.scalar.copy, 1, x1b, T // 2, T, T // 2)
         lay(nc.scalar.copy, 2, x2a, 0, T // 2, 0)
         lay(nc.scalar.copy, 2, x2b, T // 2, T, T // 2)
-        word_tile(0, 0, 4 * G, keep, "w0a")
-        word_tile(1, 0, G, keep, "w1a")
+        word_tile(0, 0, 18 * C, keep, "w0a")
+        word_tile(1, 0, 2 * G, keep, "w1a")
         word_tile(2, 0, S, keep, "w2")
-        gather_words(0, 0, 2 * G)
-        gather_words(0, 2 * G, 4 * G)
+        gather_words(0, 0, 9 * C)
+        gather_words(0, 9 * C, 18 * C)
         quantise(1, 0, 512)
         quantise(1, 512, 640)
-        word_tile(0, 4 * G, S, hold, "hold1")
-        gather_words(0, 4 * G, S)
+        word_tile(0, 18 * C, S, hold, "hold1")
+        gather_words(0, 18 * C, S)
         gather_words(1, 0, G)
+        gather_words(1, G, 2 * G)
         quantise(2, 0, 512)
         quantise(2, 512, 640)
-        word_tile(1, G, 2 * G, hold, "hold2")
-        gather_words(1, G, 2 * G)
-        word_tile(1, 2 * G, S, hold, "hold3")
+        word_tile(1, 2 * G, 10 * C, hold, "hold2")
+        gather_words(1, 2 * G, 10 * C)
+        word_tile(1, 10 * C, S, hold, "hold3")
 
-        gate_cols = keep.tile([P, NB, TOP], F32, name="gate_cols")
+        gate_cols = hold.tile([P, NB, TOP], F32, name="gate_cols", tag="hold4", align_bytes=64)
         for c0, c1 in ((0, 4), (4, NB)):
             bank = psum.tile([P, c1 - c0, P], F32, name="acc")
             for c in range(c0, c1):
@@ -201,7 +193,8 @@ def tile_moe_tk_lin_gelu_kernel(
         w_s8 = w_s[:].bitcast(U8)
 
         def multiply(e, acc, passes):
-            h, el = divmod(e, EH)
+            h = max(0, e // 4 - 1)
+            el = e - parts[h][0]
             cols = slice(e * C, (e + 1) * C)
             for a in passes:
                 if a == 0:
@@ -222,7 +215,7 @@ def tile_moe_tk_lin_gelu_kernel(
 
         def first_two(e0):
             if e0 >= 8:
-                gather_words(1, e0 * C, (e0 + 4) * C)
+                gather_words(1, max(e0, 10) * C, (e0 + 4) * C)
             for e in range(e0, e0 + 4):
                 accs[e] = psum.tile([P, C], F32, name="acc")
                 multiply(e, accs[e][:], (0, 1))
@@ -235,10 +228,14 @@ def tile_moe_tk_lin_gelu_kernel(
 
         gather_bytes(0, 2 * G)
         move_plane(0, 2 * G)
+        load_weights(2)
         first_two(0)
         first_two(4)
         gather_bytes(2 * G, S)
         move_plane(2 * G, S)
+        load_weights(3)
+        for r, pos in enumerate((pos1, pos2, pos3, pos4)):
+            nc.sync.dma_start(pos_sb[r][:], pos)
         third(0, 4)
         first_two(8)
         third(4, 8)

@@ -21,7 +21,7 @@ PASSES = 3
 S = E * C
 FLOPS = 2 * S * K * N
 
-WINS = (1536, 704, 704)
+TAIL = 896
 WIN_BYTES = 2048
 NB = T // P
 G = 4 * C
@@ -64,22 +64,22 @@ def tile_moe_tk_lin_gelu_kernel(
         tiny2 = keep.tile([P, 8], F32, name="tiny2")
         nc.gpsimd.memset(tiny[:], 0.0)
         nc.scalar.activation(out=tiny2[:], in_=tiny[:], func=GELU)
-        codes = [keep.tile([P, WINS[a]], I32, name=f"codes{a}", align_bytes=64) for a in range(PASSES)]
+        codes_all = keep.tile([P, PASSES * T + TAIL], I32, name="codes_all", align_bytes=64)
+        codes = [codes_all[:, (PASSES - 1 - a) * T :] for a in range(PASSES)]
         bytes_i32 = keep.tile([P, WIN_BYTES // 4], I32, name="bytes_i32", align_bytes=64)
         bytes_all = bytes_i32[:].bitcast(U8)
         nc.vector.memset(bytes_i32[:], 0)
-        for a in range(PASSES):
-            nc.vector.memset(codes[a][:, T:], 0)
+        nc.vector.memset(codes[0][:, T:], 0)
         w_s = keep.tile([P, 3 * E * N // 4], I32, name="w_s", align_bytes=64)
         g_moved = keep.tile([P, S // 4], I32, name="g_moved", align_bytes=64)
         nc.vector.memset(w_s[:], 0)
-        nc.gpsimd.memset(g_moved[:], 0)
+        nc.vector.memset(g_moved[:], 0)
         ident = keep.tile([P, P], F32, name="ident")
         make_identity(nc, ident[:])
-        gate_rows = keep.tile([P, T], F32, name="gate_rows")
-        nc.gpsimd.memset(gate_rows[:], 0.0)
+        gate_rows = keep.tile([P, P], F32, name="gate_rows")
+        nc.vector.memset(gate_rows[:], 0.0)
 
-        nc.sync.dma_start(out=gate_rows[0:TOP, :], in_=gate[:, 0, :])
+        nc.sync.dma_start(out=gate_rows[0 : TOP * NB, :], in_=gate[:, 0, :].rearrange("r (c p) -> r c p", p=P))
 
         b_sb = keep.tile([P, E], F32, name="b_sb")
         nc.sync.dma_start(out=b_sb[:], in_=b)
@@ -131,8 +131,9 @@ def tile_moe_tk_lin_gelu_kernel(
             return [t[:, s0 - t0 : s1 - t0] for t0, t1, t in words[a] if t0 <= s0 and s1 <= t1][0]
 
         def gather_words(a, s0, s1):
+            win = max(704, (s1 - s0) * 4 // 3)
             nc.vector.tensor_copy(
-                out=word_cols(a, s0, s1), in_=codes[a][:].bitcast(U32).indirect(offs_sb[:, s0 // 16 : s1 // 16])
+                out=word_cols(a, s0, s1), in_=codes[a][:, 0:win].bitcast(U32).indirect(offs_sb[:, s0 // 16 : s1 // 16])
             )
 
         def gather_bytes(s0, s1):
@@ -141,21 +142,21 @@ def tile_moe_tk_lin_gelu_kernel(
         def move_plane(s0, s1):
             nc.sync.dma_start(out=g_moved[0 : P - 8, s0 // 4 : s1 // 4], in_=g_bytes[8:P, s0:s1].bitcast(I32))
 
-        lay(nc.vector.tensor_copy, 0, x0a, 0, 192, 0)
-        lay(nc.scalar.copy, 0, x0a, 192, 256, 0)
+        lay(nc.vector.tensor_copy, 0, x0a, 0, 128, 0)
+        lay(nc.scalar.copy, 0, x0a, 128, 256, 0)
         quantise(0, 0, 256)
         lay(nc.vector.tensor_copy, 0, x0b, 256, 416, 256)
         lay(nc.scalar.copy, 0, x0b, 416, 512, 256)
+        quantise(0, 256, 512)
         lay(nc.vector.tensor_copy, 0, x0c, 512, 608, 512)
         lay(nc.scalar.copy, 0, x0c, 608, 640, 512)
-        quantise(0, 256, 512)
         quantise(0, 512, 640)
         lay(nc.scalar.copy, 1, x1a, 0, T // 2, 0)
         lay(nc.scalar.copy, 1, x1b, T // 2, T, T // 2)
         lay(nc.scalar.copy, 2, x2a, 0, T // 2, 0)
         lay(nc.scalar.copy, 2, x2b, T // 2, T, T // 2)
         word_tile(0, 0, 18 * C, keep, "w0a")
-        word_tile(1, 0, 2 * G, keep, "w1a")
+        word_tile(1, 0, 3 * G, keep, "w1a")
         word_tile(2, 0, S, keep, "w2")
         gather_words(0, 0, 9 * C)
         gather_words(0, 9 * C, 18 * C)
@@ -163,28 +164,24 @@ def tile_moe_tk_lin_gelu_kernel(
         quantise(1, 512, 640)
         word_tile(0, 18 * C, S, hold, "hold1")
         gather_words(0, 18 * C, S)
-        gather_words(1, 0, G)
-        gather_words(1, G, 2 * G)
+        gather_words(1, 0, 3 * G)
         quantise(2, 0, 512)
         quantise(2, 512, 640)
-        word_tile(1, 2 * G, 10 * C, hold, "hold2")
-        gather_words(1, 2 * G, 10 * C)
-        word_tile(1, 10 * C, S, hold, "hold3")
+        word_tile(1, 3 * G, 14 * C, hold, "hold2")
+        gather_words(1, 3 * G, 14 * C)
+        word_tile(1, 14 * C, S, hold, "hold3")
 
-        gate_cols = hold.tile([P, NB, TOP], F32, name="gate_cols", tag="hold4", align_bytes=64)
-        for c0, c1 in ((0, 4), (4, NB)):
-            bank = psum.tile([P, c1 - c0, P], F32, name="acc")
-            for c in range(c0, c1):
-                nc.tensor.transpose(bank[:, c - c0, :], gate_rows[:, c * P : (c + 1) * P], ident[:])
-            nc.scalar.copy(out=gate_cols[:, c0:c1, :], in_=bank[:, :, 0:TOP])
+        gate_cols = hold.tile([P, TOP * NB], F32, name="gate_cols", tag="hold4", align_bytes=64)
+        bank = psum.tile([P, P], F32, name="acc")
+        nc.tensor.transpose(bank[:], gate_rows[:], ident[:])
+        nc.scalar.copy(out=gate_cols[:], in_=bank[:, 0 : TOP * NB])
         gate_sb = keep.tile([P, TOP, T], F32, name="gate_sb")
         gate_flat = gate_sb[:].rearrange("p r t -> p (r t)")
         for j0 in range(0, TOP * NB, 4):
             bank = psum.tile([P, 4 * P], F32, name="acc")
             for j in range(j0, j0 + 4):
-                r, c = divmod(j, NB)
                 nc.tensor.transpose(
-                    bank[:, (j - j0) * P : (j - j0 + 1) * P], gate_cols[:, c, r : r + 1].to_broadcast([P, P]), ident[:]
+                    bank[:, (j - j0) * P : (j - j0 + 1) * P], gate_cols[:, j : j + 1].to_broadcast([P, P]), ident[:]
                 )
             nc.scalar.copy(out=gate_flat[:, j0 * P : (j0 + 4) * P], in_=bank[:])
 
@@ -214,8 +211,8 @@ def tile_moe_tk_lin_gelu_kernel(
         accs = {}
 
         def first_two(e0):
-            if e0 >= 8:
-                gather_words(1, max(e0, 10) * C, (e0 + 4) * C)
+            if e0 >= 12:
+                gather_words(1, max(e0, 14) * C, (e0 + 4) * C)
             for e in range(e0, e0 + 4):
                 accs[e] = psum.tile([P, C], F32, name="acc")
                 multiply(e, accs[e][:], (0, 1))

@@ -47,18 +47,16 @@ def tile_moe_tk_lin_gelu_kernel(
         x0a = keep.tile([P, 4, 256], F32, name="x0a")
         x0b = keep.tile([P, 4, 256], F32, name="x0b")
         x0c = keep.tile([P, 4, 128], F32, name="x0c")
-        x1a = keep.tile([P, 4, T // 2], F32, name="x1a")
+        x1a = hold.tile([P, 4, T // 2], F32, name="x1a", tag="hold4", align_bytes=64)
         x1b = hold.tile([P, 4, T // 2], F32, name="x1b", tag="hold1", align_bytes=64)
-        x2a = hold.tile([P, 4, T // 2], F32, name="x2a", tag="hold4", align_bytes=64)
-        x2b = hold.tile([P, 4, T // 2], F32, name="x2b", tag="hold2", align_bytes=64)
+        x2 = hold.tile([P, 4, T], F32, name="x2", tag="hold2", align_bytes=64)
         nc.sync.dma_start(out=x0a[:], in_=x_rows(0)[:, :, 0:256])
         nc.sync.dma_start(out=x0b[:], in_=x_rows(0)[:, :, 256:512])
         nc.sync.dma_start(out=x0c[:], in_=x_rows(0)[:, :, 512:640])
         nc.sync.dma_start(offs_sb[:], offs)
         nc.sync.dma_start(out=x1a[:], in_=x_rows(1)[:, :, 0 : T // 2])
         nc.sync.dma_start(out=x1b[:], in_=x_rows(1)[:, :, T // 2 : T])
-        nc.sync.dma_start(out=x2a[:], in_=x_rows(2)[:, :, 0 : T // 2])
-        nc.sync.dma_start(out=x2b[:], in_=x_rows(2)[:, :, T // 2 : T])
+        nc.sync.dma_start(out=x2[:], in_=x_rows(2))
 
         tiny = keep.tile([P, 8], F32, name="tiny")
         tiny2 = keep.tile([P, 8], F32, name="tiny2")
@@ -89,19 +87,23 @@ def tile_moe_tk_lin_gelu_kernel(
         nc.sync.dma_start(out=stage[0:P:8, E:, :], in_=w4_scales.bitcast(I32).rearrange("e a q n -> q (e a) n"))
         parts = ((0, 8), (8, 12), (12, 16), (16, E))
         w8 = [keep.tile([P, e1 - e0, N], I32, name=f"w8_{e0}", align_bytes=64) for e0, e1 in parts]
-        w4 = [keep.tile([P, e1 - e0, 2, N // 2], I32, name=f"w4_{e0}", align_bytes=64) for e0, e1 in parts]
+        w4 = [keep.tile([P, e1 - e0, N // 2], I32, name=f"w4_{e0}", align_bytes=64) for e0, e1 in parts]
+        last_parts = ((0, 8), (8, 12), (12, E))
+        w4_last = [keep.tile([P, e1 - e0, N // 2], I32, name=f"w4_last_{e0}", align_bytes=64) for e0, e1 in last_parts]
 
         def load_weights(h):
             e0, e1 = parts[h]
             nc.sync.dma_start(out=w8[h][:], in_=w8_words[e0:e1].rearrange("e a p n r -> p (e a) (n r)").bitcast(I32))
-            nc.sync.dma_start(
-                out=w4[h][:].rearrange("p e a n -> p (e a) n"),
-                in_=w4_words[e0:e1].rearrange("e a p n -> p (e a) n").bitcast(I32),
-            )
+            nc.sync.dma_start(out=w4[h][:], in_=w4_words[e0:e1, 0].rearrange("e p n -> p e n").bitcast(I32))
+
+        def load_last(h):
+            e0, e1 = last_parts[h]
+            nc.sync.dma_start(out=w4_last[h][:], in_=w4_words[e0:e1, 1].rearrange("e p n -> p e n").bitcast(I32))
 
         load_weights(0)
         for r in range(4):
             nc.sync.dma_start(out=w_s[r:P:32, :], in_=stage[8 * r : P : 32, :, :].rearrange("p g n -> p (g n)"))
+        load_last(0)
         load_weights(1)
 
         xb = [keep.tile([P, T, 4], BF16, name=f"xb{a}", align_bytes=64) for a in range(2)]
@@ -131,7 +133,7 @@ def tile_moe_tk_lin_gelu_kernel(
             return [t[:, s0 - t0 : s1 - t0] for t0, t1, t in words[a] if t0 <= s0 and s1 <= t1][0]
 
         def gather_words(a, s0, s1):
-            win = max(704, (s1 - s0) * 4 // 3)
+            win = max(704, (s1 - s0) * 3 // 2 if a else (s1 - s0) * 4 // 3)
             nc.vector.tensor_copy(
                 out=word_cols(a, s0, s1), in_=codes[a][:, 0:win].bitcast(U32).indirect(offs_sb[:, s0 // 16 : s1 // 16])
             )
@@ -153,10 +155,10 @@ def tile_moe_tk_lin_gelu_kernel(
         quantise(0, 512, 640)
         lay(nc.scalar.copy, 1, x1a, 0, T // 2, 0)
         lay(nc.scalar.copy, 1, x1b, T // 2, T, T // 2)
-        lay(nc.scalar.copy, 2, x2a, 0, T // 2, 0)
-        lay(nc.scalar.copy, 2, x2b, T // 2, T, T // 2)
+        lay(nc.scalar.copy, 2, x2, 0, 512, 0)
+        lay(nc.scalar.copy, 2, x2, 512, T, 0)
         word_tile(0, 0, 18 * C, keep, "w0a")
-        word_tile(1, 0, 3 * G, keep, "w1a")
+        word_tile(1, 0, 10 * C, keep, "w1a")
         word_tile(2, 0, S, keep, "w2")
         gather_words(0, 0, 9 * C)
         gather_words(0, 9 * C, 18 * C)
@@ -164,12 +166,12 @@ def tile_moe_tk_lin_gelu_kernel(
         quantise(1, 512, 640)
         word_tile(0, 18 * C, S, hold, "hold1")
         gather_words(0, 18 * C, S)
-        gather_words(1, 0, 3 * G)
+        gather_words(1, 0, 10 * C)
         quantise(2, 0, 512)
         quantise(2, 512, 640)
-        word_tile(1, 3 * G, 14 * C, hold, "hold2")
-        gather_words(1, 3 * G, 14 * C)
-        word_tile(1, 14 * C, S, hold, "hold3")
+        word_tile(1, 10 * C, 12 * C, hold, "hold2")
+        gather_words(1, 10 * C, 12 * C)
+        word_tile(1, 12 * C, S, hold, "hold3")
 
         gate_cols = hold.tile([P, TOP * NB], F32, name="gate_cols", tag="hold4", align_bytes=64)
         bank = psum.tile([P, P], F32, name="acc")
@@ -198,7 +200,9 @@ def tile_moe_tk_lin_gelu_kernel(
                     lhs, lhs_scale, plane = w8[h][:, el, :].bitcast(FP8X4), w_s8[:, e * N : (e + 1) * N], g_bytes[4:P, cols]
                 else:
                     g = E + 2 * e + a - 1
-                    lhs, lhs_scale = w4[h][:, el, a - 1, :].bitcast(FP4X4), w_s8[:, g * N : (g + 1) * N]
+                    hl = min(h, 2)
+                    packed = w4[h][:, el, :] if a == 1 else w4_last[hl][:, e - last_parts[hl][0], :]
+                    lhs, lhs_scale = packed.bitcast(FP4X4), w_s8[:, g * N : (g + 1) * N]
                     plane = g_bytes[:, cols] if a == 1 else moved8[:, cols]
                 nc.tensor.matmul_mx(
                     out=acc, lhsT=lhs, lhsT_scale=lhs_scale, rhs=word_cols(a, e * C, (e + 1) * C).bitcast(FP8X4), rhs_scale=plane,
@@ -212,7 +216,7 @@ def tile_moe_tk_lin_gelu_kernel(
 
         def first_two(e0):
             if e0 >= 12:
-                gather_words(1, max(e0, 14) * C, (e0 + 4) * C)
+                gather_words(1, e0 * C, (e0 + 4) * C)
             for e in range(e0, e0 + 4):
                 accs[e] = psum.tile([P, C], F32, name="acc")
                 multiply(e, accs[e][:], (0, 1))
@@ -230,7 +234,9 @@ def tile_moe_tk_lin_gelu_kernel(
         first_two(4)
         gather_bytes(2 * G, S)
         move_plane(2 * G, S)
+        load_last(1)
         load_weights(3)
+        load_last(2)
         for r, pos in enumerate((pos1, pos2, pos3, pos4)):
             nc.sync.dma_start(pos_sb[r][:], pos)
         third(0, 4)
@@ -244,7 +250,7 @@ def tile_moe_tk_lin_gelu_kernel(
         third(18, 19)
         third(19, 20)
 
-        halves = ((0, 3), (3, NB))
+        thirds = ((0, 2), (2, 4), (4, NB))
         prod = [keep.tile([P, T], F32, name=f"prod{r}") for r in range(TOP)]
         res = keep.tile([P, T], F32, name="res")
         turned = [keep.tile([P, P], F32, name=f"turned{c}") for c in range(NB)]
@@ -275,10 +281,10 @@ def tile_moe_tk_lin_gelu_kernel(
 
         fetch(0, 0, NB)
         fetch(1, 0, NB)
-        for c0, c1 in halves:
+        for c0, c1 in thirds:
             fetch(2, c0, c1)
             turn_back(c0, c1)
-        for c0, c1 in halves:
-            fetch(3, c0, c1)
-        for c0, c1 in halves:
+        fetch(3, 0, 4)
+        fetch(3, 4, NB)
+        for c0, c1 in thirds:
             finish(c0, c1)

@@ -227,23 +227,22 @@ def tile_moe_tk_lin_gelu_kernel(
                 multiply(e, accs[e][:], (2,))
                 activate(e, accs[e][:])
 
-        gather_bytes(0, 2 * G)
-        move_plane(0, 2 * G)
+        gather_bytes(0, 3 * G)
+        move_plane(0, 3 * G)
         load_weights(2)
-        first_two(0)
-        first_two(4)
-        gather_bytes(2 * G, S)
-        move_plane(2 * G, S)
         load_last(1)
         load_weights(3)
         load_last(2)
         for r, pos in enumerate((pos1, pos2, pos3, pos4)):
             nc.sync.dma_start(pos_sb[r][:], pos)
-        third(0, 4)
+        first_two(0)
+        first_two(4)
+        third(0, 8)
         first_two(8)
-        third(4, 8)
-        first_two(12)
+        gather_bytes(3 * G, S)
+        move_plane(3 * G, S)
         third(8, 12)
+        first_two(12)
         first_two(16)
         third(12, 16)
         third(16, 18)

@@ -21,10 +21,13 @@ PASSES = 3
 S = E * C
 FLOPS = 2 * S * K * N
 
-TAIL = 896
-WIN_BYTES = 2048
+BANKS = 8
+GROUP = 4
 NB = T // P
-G = 4 * C
+PER_COLUMN = 16
+TAIL = 896
+WINDOW_LEAST = T + 64
+WINDOW_BYTES = 2048
 PLANE = (4, 0, 8)
 
 
@@ -36,10 +39,10 @@ def tile_moe_tk_lin_gelu_kernel(
         lists = ctx.enter_context(tc.tile_pool(name="lists", bufs=1))
         keep = ctx.enter_context(tc.tile_pool(name="keep", bufs=1))
         hold = ctx.enter_context(tc.tile_pool(name="hold", bufs=1))
-        psum = ctx.enter_context(tc.psum_pool(name="psum", bufs=8))
+        psum = ctx.enter_context(tc.psum_pool(name="psum", bufs=BANKS))
 
-        offs_sb = lists.tile([P, S // 16], U16, name="offs_sb")
-        pos_sb = [lists.tile([P, T // 16], U16, name=f"pos{r}_sb") for r in range(TOP)]
+        offs_sb = lists.tile([P, S // PER_COLUMN], U16, name="offs_sb")
+        pos_sb = [lists.tile([P, T // PER_COLUMN], U16, name=f"pos{r}_sb") for r in range(TOP)]
 
         def x_rows(a):
             return xT[512 * a : 512 * (a + 1), :].rearrange("(p j) t -> p j t", j=4)
@@ -52,238 +55,241 @@ def tile_moe_tk_lin_gelu_kernel(
         x2 = hold.tile([P, 4, T], F32, name="x2", tag="hold2", align_bytes=64)
         nc.sync.dma_start(out=x0a[:], in_=x_rows(0)[:, :, 0:256])
         nc.sync.dma_start(out=x0b[:], in_=x_rows(0)[:, :, 256:512])
-        nc.sync.dma_start(out=x0c[:], in_=x_rows(0)[:, :, 512:640])
+        nc.sync.dma_start(out=x0c[:], in_=x_rows(0)[:, :, 512:T])
         nc.sync.dma_start(offs_sb[:], offs)
         nc.sync.dma_start(out=x1a[:], in_=x_rows(1)[:, :, 0 : T // 2])
         nc.sync.dma_start(out=x1b[:], in_=x_rows(1)[:, :, T // 2 : T])
         nc.sync.dma_start(out=x2[:], in_=x_rows(2))
 
-        tiny = keep.tile([P, 8], F32, name="tiny")
-        tiny2 = keep.tile([P, 8], F32, name="tiny2")
-        nc.gpsimd.memset(tiny[:], 0.0)
-        nc.scalar.activation(out=tiny2[:], in_=tiny[:], func=GELU)
+        warm_in = keep.tile([P, 8], F32, name="tiny")
+        warm_out = keep.tile([P, 8], F32, name="tiny2")
+        nc.gpsimd.memset(warm_in[:], 0.0)
+        nc.scalar.activation(out=warm_out[:], in_=warm_in[:], func=GELU)
+
         codes_all = keep.tile([P, PASSES * T + TAIL], I32, name="codes_all", align_bytes=64)
         codes = [codes_all[:, (PASSES - 1 - a) * T :] for a in range(PASSES)]
-        bytes_i32 = keep.tile([P, WIN_BYTES // 4], I32, name="bytes_i32", align_bytes=64)
-        bytes_all = bytes_i32[:].bitcast(U8)
-        nc.vector.memset(bytes_i32[:], 0)
+        token_scales_i32 = keep.tile([P, WINDOW_BYTES // 4], I32, name="bytes_i32", align_bytes=64)
+        token_scales = token_scales_i32[:].bitcast(U8)
+        nc.vector.memset(token_scales_i32[:], 0)
         nc.vector.memset(codes[0][:, T:], 0)
-        w_s = keep.tile([P, 3 * E * N // 4], I32, name="w_s", align_bytes=64)
-        g_moved = keep.tile([P, S // 4], I32, name="g_moved", align_bytes=64)
-        nc.vector.memset(w_s[:], 0)
-        nc.vector.memset(g_moved[:], 0)
+        w_scales_i32 = keep.tile([P, PASSES * E * N // 4], I32, name="w_s", align_bytes=64)
+        moved_i32 = keep.tile([P, S // 4], I32, name="g_moved", align_bytes=64)
+        nc.vector.memset(w_scales_i32[:], 0)
+        nc.vector.memset(moved_i32[:], 0)
         ident = keep.tile([P, P], F32, name="ident")
         make_identity(nc, ident[:])
+
         gate_rows = keep.tile([P, P], F32, name="gate_rows")
         nc.vector.memset(gate_rows[:], 0.0)
-
         nc.sync.dma_start(out=gate_rows[0 : TOP * NB, :], in_=gate[:, 0, :].rearrange("r (c p) -> r c p", p=P))
-
         b_sb = keep.tile([P, E], F32, name="b_sb")
         nc.sync.dma_start(out=b_sb[:], in_=b)
 
-        stage = keep.tile([P, 3 * E, N // 4], I32, name="stage")
+        stage = keep.tile([P, PASSES * E, N // 4], I32, name="stage")
         nc.sync.dma_start(out=stage[0:P:8, 0:E, :], in_=w8_scales.bitcast(I32).rearrange("e a q n -> q (e a) n"))
         nc.sync.dma_start(out=stage[0:P:8, E:, :], in_=w4_scales.bitcast(I32).rearrange("e a q n -> q (e a) n"))
-        parts = ((0, 8), (8, 12), (12, 16), (16, E))
-        w8 = [keep.tile([P, e1 - e0, N], I32, name=f"w8_{e0}", align_bytes=64) for e0, e1 in parts]
-        w4 = [keep.tile([P, e1 - e0, N // 2], I32, name=f"w4_{e0}", align_bytes=64) for e0, e1 in parts]
-        last_parts = ((0, 8), (8, 12), (12, E))
-        w4_last = [keep.tile([P, e1 - e0, N // 2], I32, name=f"w4_last_{e0}", align_bytes=64) for e0, e1 in last_parts]
+        open_parts = ((0, 8), (8, 12), (12, 16), (16, E))
+        w_pass0 = [keep.tile([P, e1 - e0, N], I32, name=f"w8_{e0}", align_bytes=64) for e0, e1 in open_parts]
+        w_pass1 = [keep.tile([P, e1 - e0, N // 2], I32, name=f"w4_{e0}", align_bytes=64) for e0, e1 in open_parts]
+        close_parts = ((0, 8), (8, 12), (12, E))
+        w_pass2 = [keep.tile([P, e1 - e0, N // 2], I32, name=f"w4_last_{e0}", align_bytes=64) for e0, e1 in close_parts]
 
-        def load_weights(h):
-            e0, e1 = parts[h]
-            nc.sync.dma_start(out=w8[h][:], in_=w8_words[e0:e1].rearrange("e a p n r -> p (e a) (n r)").bitcast(I32))
-            nc.sync.dma_start(out=w4[h][:], in_=w4_words[e0:e1, 0].rearrange("e p n -> p e n").bitcast(I32))
+        def load_opening(h):
+            e0, e1 = open_parts[h]
+            nc.sync.dma_start(out=w_pass0[h][:], in_=w8_words[e0:e1].rearrange("e a p n r -> p (e a) (n r)").bitcast(I32))
+            nc.sync.dma_start(out=w_pass1[h][:], in_=w4_words[e0:e1, 0].rearrange("e p n -> p e n").bitcast(I32))
 
-        def load_last(h):
-            e0, e1 = last_parts[h]
-            nc.sync.dma_start(out=w4_last[h][:], in_=w4_words[e0:e1, 1].rearrange("e p n -> p e n").bitcast(I32))
+        def load_closing(h):
+            e0, e1 = close_parts[h]
+            nc.sync.dma_start(out=w_pass2[h][:], in_=w4_words[e0:e1, 1].rearrange("e p n -> p e n").bitcast(I32))
 
-        load_weights(0)
+        def expert_words(parts, tiles, e):
+            return [t[:, e - e0, :] for (e0, e1), t in zip(parts, tiles) if e0 <= e < e1][0]
+
+        load_opening(0)
         for r in range(4):
-            nc.sync.dma_start(out=w_s[r:P:32, :], in_=stage[8 * r : P : 32, :, :].rearrange("p g n -> p (g n)"))
-        load_last(0)
-        load_weights(1)
+            nc.sync.dma_start(out=w_scales_i32[r:P:32, :], in_=stage[8 * r : P : 32, :, :].rearrange("p g n -> p (g n)"))
+        load_closing(0)
+        load_opening(1)
 
         xb = [keep.tile([P, T, 4], BF16, name=f"xb{a}", align_bytes=64) for a in range(2)]
         xb.append(hold.tile([P, T, 4], BF16, name="xb2", tag="hold3", align_bytes=64))
 
-        def lay(copy, a, src, c0, c1, s0):
+        def round_tokens(copy, a, src, t0, t1, src_t0):
             copy(
-                out=xb[a][:, c0:c1, :].rearrange("p (c i) j -> p c j i", i=4),
-                in_=src[:, :, c0 - s0 : c1 - s0].rearrange("p j (c i) -> p c j i", i=4),
+                out=xb[a][:, t0:t1, :].rearrange("p (c i) j -> p c j i", i=4),
+                in_=src[:, :, t0 - src_t0 : t1 - src_t0].rearrange("p j (c i) -> p c j i", i=4),
             )
 
-        def quantise(a, c0, c1):
-            k = PLANE[a]
+        def quantise(a, t0, t1):
             nc.vector.quantize_mx(
-                out=codes[a][:, c0:c1].bitcast(FP8X4),
-                scales=bytes_all[k:P, c0:c1],
-                in_=xb[a][:, c0:c1, :].rearrange("p n j -> p (n j)"),
+                out=codes[a][:, t0:t1].bitcast(FP8X4),
+                scales=token_scales[PLANE[a] : P, t0:t1],
+                in_=xb[a][:, t0:t1, :].rearrange("p n j -> p (n j)"),
             )
 
-        words = {a: [] for a in range(PASSES)}
-        g_bytes = keep.tile([P, S], U8, name="g_bytes", align_bytes=64)
+        slot_words = {a: [] for a in range(PASSES)}
+        slot_scales = keep.tile([P, S], U8, name="g_bytes", align_bytes=64)
 
-        def word_tile(a, s0, s1, pool, tag):
-            words[a].append((s0, s1, pool.tile([P, s1 - s0], U32, name=f"words{a}_{s0}", tag=tag, align_bytes=64)))
+        def word_tile(a, e0, e1, pool, tag):
+            tile_words = pool.tile([P, (e1 - e0) * C], U32, name=f"words{a}_{e0 * C}", tag=tag, align_bytes=64)
+            slot_words[a].append((e0, e1, tile_words))
 
-        def word_cols(a, s0, s1):
-            return [t[:, s0 - t0 : s1 - t0] for t0, t1, t in words[a] if t0 <= s0 and s1 <= t1][0]
+        def word_cols(a, e0, e1):
+            return [t[:, (e0 - f0) * C : (e1 - f0) * C] for f0, f1, t in slot_words[a] if f0 <= e0 and e1 <= f1][0]
 
-        def gather_words(a, s0, s1):
-            win = max(704, (s1 - s0) * 3 // 2 if a else (s1 - s0) * 4 // 3)
-            nc.vector.tensor_copy(
-                out=word_cols(a, s0, s1), in_=codes[a][:, 0:win].bitcast(U32).indirect(offs_sb[:, s0 // 16 : s1 // 16])
+        def slot_list(e0, e1):
+            return offs_sb[:, e0 * C // PER_COLUMN : e1 * C // PER_COLUMN]
+
+        def gather_words(a, e0, e1):
+            count = (e1 - e0) * C
+            window = max(WINDOW_LEAST, count * 3 // 2 if a else count * 4 // 3)
+            nc.vector.tensor_copy(out=word_cols(a, e0, e1), in_=codes[a][:, 0:window].bitcast(U32).indirect(slot_list(e0, e1)))
+
+        def gather_scales(e0, e1):
+            nc.vector.tensor_copy(out=slot_scales[:, e0 * C : e1 * C], in_=token_scales.indirect(slot_list(e0, e1)))
+            nc.sync.dma_start(
+                out=moved_i32[0 : P - PLANE[2], e0 * C // 4 : e1 * C // 4],
+                in_=slot_scales[PLANE[2] : P, e0 * C : e1 * C].bitcast(I32),
             )
 
-        def gather_bytes(s0, s1):
-            nc.vector.tensor_copy(out=g_bytes[:, s0:s1], in_=bytes_all.indirect(offs_sb[:, s0 // 16 : s1 // 16]))
-
-        def move_plane(s0, s1):
-            nc.sync.dma_start(out=g_moved[0 : P - 8, s0 // 4 : s1 // 4], in_=g_bytes[8:P, s0:s1].bitcast(I32))
-
-        lay(nc.vector.tensor_copy, 0, x0a, 0, 128, 0)
-        lay(nc.scalar.copy, 0, x0a, 128, 256, 0)
+        round_tokens(nc.vector.tensor_copy, 0, x0a, 0, 128, 0)
+        round_tokens(nc.scalar.copy, 0, x0a, 128, 256, 0)
         quantise(0, 0, 256)
-        lay(nc.vector.tensor_copy, 0, x0b, 256, 416, 256)
-        lay(nc.scalar.copy, 0, x0b, 416, 512, 256)
+        round_tokens(nc.vector.tensor_copy, 0, x0b, 256, 416, 256)
+        round_tokens(nc.scalar.copy, 0, x0b, 416, 512, 256)
         quantise(0, 256, 512)
-        lay(nc.vector.tensor_copy, 0, x0c, 512, 608, 512)
-        lay(nc.scalar.copy, 0, x0c, 608, 640, 512)
-        quantise(0, 512, 640)
-        lay(nc.scalar.copy, 1, x1a, 0, T // 2, 0)
-        lay(nc.scalar.copy, 1, x1b, T // 2, T, T // 2)
-        lay(nc.scalar.copy, 2, x2, 0, 512, 0)
-        lay(nc.scalar.copy, 2, x2, 512, T, 0)
-        word_tile(0, 0, 18 * C, keep, "w0a")
-        word_tile(1, 0, 10 * C, keep, "w1a")
-        word_tile(2, 0, S, keep, "w2")
-        gather_words(0, 0, 9 * C)
-        gather_words(0, 9 * C, 18 * C)
+        round_tokens(nc.vector.tensor_copy, 0, x0c, 512, 608, 512)
+        round_tokens(nc.scalar.copy, 0, x0c, 608, T, 512)
+        quantise(0, 512, T)
+        round_tokens(nc.scalar.copy, 1, x1a, 0, T // 2, 0)
+        round_tokens(nc.scalar.copy, 1, x1b, T // 2, T, T // 2)
+        round_tokens(nc.scalar.copy, 2, x2, 0, 512, 0)
+        round_tokens(nc.scalar.copy, 2, x2, 512, T, 0)
+
+        word_tile(0, 0, 18, keep, "w0a")
+        word_tile(1, 0, 10, keep, "w1a")
+        word_tile(2, 0, E, keep, "w2")
+        gather_words(0, 0, 9)
+        gather_words(0, 9, 18)
         quantise(1, 0, 512)
-        quantise(1, 512, 640)
-        word_tile(0, 18 * C, S, hold, "hold1")
-        gather_words(0, 18 * C, S)
-        gather_words(1, 0, 10 * C)
+        quantise(1, 512, T)
+        word_tile(0, 18, E, hold, "hold1")
+        gather_words(0, 18, E)
+        gather_words(1, 0, 10)
         quantise(2, 0, 512)
-        quantise(2, 512, 640)
-        word_tile(1, 10 * C, 12 * C, hold, "hold2")
-        gather_words(1, 10 * C, 12 * C)
-        word_tile(1, 12 * C, S, hold, "hold3")
+        quantise(2, 512, T)
+        word_tile(1, 10, 12, hold, "hold2")
+        gather_words(1, 10, 12)
+        word_tile(1, 12, E, hold, "hold3")
 
         gate_cols = hold.tile([P, TOP * NB], F32, name="gate_cols", tag="hold4", align_bytes=64)
-        bank = psum.tile([P, P], F32, name="acc")
-        nc.tensor.transpose(bank[:], gate_rows[:], ident[:])
-        nc.scalar.copy(out=gate_cols[:], in_=bank[:, 0 : TOP * NB])
+        turned_gate = psum.tile([P, P], F32, name="acc")
+        nc.tensor.transpose(turned_gate[:], gate_rows[:], ident[:])
+        nc.scalar.copy(out=gate_cols[:], in_=turned_gate[:, 0 : TOP * NB])
         gate_sb = keep.tile([P, TOP, T], F32, name="gate_sb")
         gate_flat = gate_sb[:].rearrange("p r t -> p (r t)")
         for j0 in range(0, TOP * NB, 4):
-            bank = psum.tile([P, 4 * P], F32, name="acc")
+            spread = psum.tile([P, 4 * P], F32, name="acc")
             for j in range(j0, j0 + 4):
                 nc.tensor.transpose(
-                    bank[:, (j - j0) * P : (j - j0 + 1) * P], gate_cols[:, j : j + 1].to_broadcast([P, P]), ident[:]
+                    spread[:, (j - j0) * P : (j - j0 + 1) * P], gate_cols[:, j : j + 1].to_broadcast([P, P]), ident[:]
                 )
-            nc.scalar.copy(out=gate_flat[:, j0 * P : (j0 + 4) * P], in_=bank[:])
+            nc.scalar.copy(out=gate_flat[:, j0 * P : (j0 + 4) * P], in_=spread[:])
 
         y = keep.tile([P, S], F32, name="y")
-        moved8 = g_moved[:].bitcast(U8)
-        w_s8 = w_s[:].bitcast(U8)
+        moved_scales = moved_i32[:].bitcast(U8)
+        w_scales = w_scales_i32[:].bitcast(U8)
+        sums = {}
 
-        def multiply(e, acc, passes):
-            h = max(0, e // 4 - 1)
-            el = e - parts[h][0]
+        def multiply(e, a):
             cols = slice(e * C, (e + 1) * C)
-            for a in passes:
-                if a == 0:
-                    lhs, lhs_scale, plane = w8[h][:, el, :].bitcast(FP8X4), w_s8[:, e * N : (e + 1) * N], g_bytes[4:P, cols]
-                else:
-                    g = E + 2 * e + a - 1
-                    hl = min(h, 2)
-                    packed = w4[h][:, el, :] if a == 1 else w4_last[hl][:, e - last_parts[hl][0], :]
-                    lhs, lhs_scale = packed.bitcast(FP4X4), w_s8[:, g * N : (g + 1) * N]
-                    plane = g_bytes[:, cols] if a == 1 else moved8[:, cols]
-                nc.tensor.matmul_mx(
-                    out=acc, lhsT=lhs, lhsT_scale=lhs_scale, rhs=word_cols(a, e * C, (e + 1) * C).bitcast(FP8X4), rhs_scale=plane,
-                    start=(a == 0), stop=(a == 2),
-                )
+            weights = (
+                expert_words(open_parts, w_pass0, e).bitcast(FP8X4),
+                expert_words(open_parts, w_pass1, e).bitcast(FP4X4),
+                expert_words(close_parts, w_pass2, e).bitcast(FP4X4),
+            )[a]
+            plane = e if a == 0 else E + 2 * e + a - 1
+            nc.tensor.matmul_mx(
+                out=sums[e][:],
+                lhsT=weights,
+                lhsT_scale=w_scales[:, plane * N : (plane + 1) * N],
+                rhs=word_cols(a, e, e + 1).bitcast(FP8X4),
+                rhs_scale=(slot_scales[PLANE[0] : P, cols], slot_scales[:, cols], moved_scales[:, cols])[a],
+                start=(a == 0),
+                stop=(a == PASSES - 1),
+            )
 
-        def activate(e, acc):
-            nc.scalar.activation(out=y[:, e * C : (e + 1) * C], in_=acc, func=GELU, bias=b_sb[:, e : e + 1])
+        def open_group(e0):
+            for e in range(e0, e0 + GROUP):
+                sums[e] = psum.tile([P, C], F32, name="acc")
+                multiply(e, 0)
+                multiply(e, 1)
 
-        accs = {}
+        def gather_and_open(e0):
+            gather_words(1, e0, e0 + GROUP)
+            open_group(e0)
 
-        def first_two(e0):
-            if e0 >= 12:
-                gather_words(1, e0 * C, (e0 + 4) * C)
-            for e in range(e0, e0 + 4):
-                accs[e] = psum.tile([P, C], F32, name="acc")
-                multiply(e, accs[e][:], (0, 1))
-
-        def third(e0, e1):
-            gather_words(2, e0 * C, e1 * C)
+        def gather_and_close(e0, e1):
+            gather_words(2, e0, e1)
             for e in range(e0, e1):
-                multiply(e, accs[e][:], (2,))
-                activate(e, accs[e][:])
+                multiply(e, 2)
+                nc.scalar.activation(out=y[:, e * C : (e + 1) * C], in_=sums[e][:], func=GELU, bias=b_sb[:, e : e + 1])
 
-        gather_bytes(0, 3 * G)
-        move_plane(0, 3 * G)
-        load_weights(2)
-        load_last(1)
-        load_weights(3)
-        load_last(2)
+        load_opening(2)
+        gather_scales(0, 12)
+        load_closing(1)
+        load_opening(3)
+        load_closing(2)
+        open_group(0)
+        open_group(4)
+        gather_and_close(0, 8)
+        open_group(8)
+        gather_scales(12, E)
         for r, pos in enumerate((pos1, pos2, pos3, pos4)):
             nc.sync.dma_start(pos_sb[r][:], pos)
-        first_two(0)
-        first_two(4)
-        third(0, 8)
-        first_two(8)
-        gather_bytes(3 * G, S)
-        move_plane(3 * G, S)
-        third(8, 12)
-        first_two(12)
-        first_two(16)
-        third(12, 16)
-        third(16, 18)
-        third(18, 19)
-        third(19, 20)
+        gather_and_open(12)
+        gather_and_close(8, 12)
+        gather_and_open(16)
+        gather_and_close(12, 16)
+        gather_and_close(16, 18)
+        gather_and_close(18, 19)
+        gather_and_close(19, E)
 
-        thirds = ((0, 2), (2, 4), (4, NB))
+        token_parts = ((0, 2), (2, 4), (4, NB))
         prod = [keep.tile([P, T], F32, name=f"prod{r}") for r in range(TOP)]
         res = keep.tile([P, T], F32, name="res")
         turned = [keep.tile([P, P], F32, name=f"turned{c}") for c in range(NB)]
-        sums = [psum.tile([P, P], F32, name="acc") for c in range(NB)]
+        three = [psum.tile([P, P], F32, name="acc") for c in range(NB)]
+        back = {}
 
         def fetch(r, c0, c1):
             cols = slice(c0 * P, c1 * P)
-            nc.vector.tensor_tensor(prod[r][:, cols], y[:].indirect(pos_sb[r][:, c0 * 8 : c1 * 8]), gate_sb[:, r, cols], MULT)
-            if r < TOP - 1:
-                for c in range(c0, c1):
-                    nc.tensor.matmul(
-                        sums[c][:], prod[r][:, c * P : (c + 1) * P], ident[:],
-                        start=(r == 0), stop=(r == TOP - 2), is_transpose=True,
-                    )
+            token_list = pos_sb[r][:, c0 * P // PER_COLUMN : c1 * P // PER_COLUMN]
+            nc.vector.tensor_tensor(prod[r][:, cols], y[:].indirect(token_list), gate_sb[:, r, cols], MULT)
 
-        back = {}
+        def fetch_and_turn(r, c0, c1):
+            fetch(r, c0, c1)
+            for c in range(c0, c1):
+                nc.tensor.matmul(
+                    three[c][:], prod[r][:, c * P : (c + 1) * P], ident[:],
+                    start=(r == 0), stop=(r == TOP - 2), is_transpose=True,
+                )
 
         def turn_back(c0, c1):
             back[c0] = psum.tile([P, (c1 - c0) * P], F32, name="acc")
             for c in range(c0, c1):
-                nc.scalar.copy(out=turned[c][:], in_=sums[c][:])
+                nc.scalar.copy(out=turned[c][:], in_=three[c][:])
                 nc.tensor.transpose(back[c0][:, (c - c0) * P : (c - c0 + 1) * P], turned[c][:], ident[:])
 
-        def finish(c0, c1):
+        fetch_and_turn(0, 0, NB)
+        fetch_and_turn(1, 0, NB)
+        for c0, c1 in token_parts:
+            fetch_and_turn(2, c0, c1)
+            turn_back(c0, c1)
+        fetch(TOP - 1, 0, NB - 1)
+        fetch(TOP - 1, NB - 1, NB)
+        for c0, c1 in token_parts:
             cols = slice(c0 * P, c1 * P)
             nc.vector.tensor_tensor(res[:, cols], prod[TOP - 1][:, cols], back[c0][:], ADD)
             nc.sync.dma_start(out=out[:, cols], in_=res[:, cols])
-
-        fetch(0, 0, NB)
-        fetch(1, 0, NB)
-        for c0, c1 in thirds:
-            fetch(2, c0, c1)
-            turn_back(c0, c1)
-        fetch(3, 0, 4)
-        fetch(3, 4, NB)
-        for c0, c1 in thirds:
-            finish(c0, c1)

@@ -22,7 +22,7 @@ S = E * C
 FLOPS = 2 * S * K * N
 
 BANKS = 8
-GROUP = 4
+BANK_EXPERTS = ((0, 4), (4, 8), (8, 12), (12, 15), (15, 17), (17, 18), (18, 19), (19, 20))
 NB = T // P
 PER_COLUMN = 16
 TAIL = 896
@@ -59,6 +59,9 @@ def tile_moe_tk_lin_gelu_kernel(
         nc.sync.dma_start(offs_sb[:], offs)
         nc.sync.dma_start(out=x1a[:], in_=x_rows(1)[:, :, 0 : T // 2])
         nc.sync.dma_start(out=x1b[:], in_=x_rows(1)[:, :, T // 2 : T])
+        stage = keep.tile([P, PASSES * E, N // 4], I32, name="stage")
+        nc.sync.dma_start(out=stage[0:P:8, 0:E, :], in_=w8_scales.bitcast(I32).rearrange("e a q n -> q (e a) n"))
+        nc.sync.dma_start(out=stage[0:P:8, E:, :], in_=w4_scales.bitcast(I32).rearrange("e a q n -> q (e a) n"))
         nc.sync.dma_start(out=x2[:], in_=x_rows(2))
 
         warm_in = keep.tile([P, 8], F32, name="tiny")
@@ -85,32 +88,14 @@ def tile_moe_tk_lin_gelu_kernel(
         b_sb = keep.tile([P, E], F32, name="b_sb")
         nc.sync.dma_start(out=b_sb[:], in_=b)
 
-        stage = keep.tile([P, PASSES * E, N // 4], I32, name="stage")
-        nc.sync.dma_start(out=stage[0:P:8, 0:E, :], in_=w8_scales.bitcast(I32).rearrange("e a q n -> q (e a) n"))
-        nc.sync.dma_start(out=stage[0:P:8, E:, :], in_=w4_scales.bitcast(I32).rearrange("e a q n -> q (e a) n"))
-        open_parts = ((0, 8), (8, 12), (12, 16), (16, E))
-        w_pass0 = [keep.tile([P, e1 - e0, N], I32, name=f"w8_{e0}", align_bytes=64) for e0, e1 in open_parts]
-        w_pass1 = [keep.tile([P, e1 - e0, N // 2], I32, name=f"w4_{e0}", align_bytes=64) for e0, e1 in open_parts]
-        close_parts = ((0, 8), (8, 12), (12, E))
-        w_pass2 = [keep.tile([P, e1 - e0, N // 2], I32, name=f"w4_last_{e0}", align_bytes=64) for e0, e1 in close_parts]
-
-        def load_opening(h):
-            e0, e1 = open_parts[h]
-            nc.sync.dma_start(out=w_pass0[h][:], in_=w8_words[e0:e1].rearrange("e a p n r -> p (e a) (n r)").bitcast(I32))
-            nc.sync.dma_start(out=w_pass1[h][:], in_=w4_words[e0:e1, 0].rearrange("e p n -> p e n").bitcast(I32))
-
-        def load_closing(h):
-            e0, e1 = close_parts[h]
-            nc.sync.dma_start(out=w_pass2[h][:], in_=w4_words[e0:e1, 1].rearrange("e p n -> p e n").bitcast(I32))
-
-        def expert_words(parts, tiles, e):
-            return [t[:, e - e0, :] for (e0, e1), t in zip(parts, tiles) if e0 <= e < e1][0]
-
-        load_opening(0)
+        w_words = [keep.tile([P, E, N // (2 if a else 1)], I32, name=f"w_pass{a}", align_bytes=64) for a in range(PASSES)]
         for r in range(4):
             nc.sync.dma_start(out=w_scales_i32[r:P:32, :], in_=stage[8 * r : P : 32, :, :].rearrange("p g n -> p (g n)"))
-        load_closing(0)
-        load_opening(1)
+        nc.sync.dma_start(out=w_words[0][:], in_=w8_words.rearrange("e a p n r -> p (e a) (n r)").bitcast(I32))
+        for a in (1, 2):
+            nc.sync.dma_start(out=w_words[a][:], in_=w4_words[:, a - 1].rearrange("e p n -> p e n").bitcast(I32))
+        for r, pos in enumerate((pos1, pos2, pos3, pos4)):
+            nc.sync.dma_start(pos_sb[r][:], pos)
 
         xb = [keep.tile([P, T, 4], BF16, name=f"xb{a}", align_bytes=64) for a in range(2)]
         xb.append(hold.tile([P, T, 4], BF16, name="xb2", tag="hold3", align_bytes=64))
@@ -148,10 +133,6 @@ def tile_moe_tk_lin_gelu_kernel(
 
         def gather_scales(e0, e1):
             nc.vector.tensor_copy(out=slot_scales[:, e0 * C : e1 * C], in_=token_scales.indirect(slot_list(e0, e1)))
-            nc.sync.dma_start(
-                out=moved_i32[0 : P - PLANE[2], e0 * C // 4 : e1 * C // 4],
-                in_=slot_scales[PLANE[2] : P, e0 * C : e1 * C].bitcast(I32),
-            )
 
         round_tokens(nc.vector.tensor_copy, 0, x0a, 0, 128, 0)
         round_tokens(nc.scalar.copy, 0, x0a, 128, 256, 0)
@@ -200,61 +181,52 @@ def tile_moe_tk_lin_gelu_kernel(
         y = keep.tile([P, S], F32, name="y")
         moved_scales = moved_i32[:].bitcast(U8)
         w_scales = w_scales_i32[:].bitcast(U8)
-        sums = {}
+        banks = [psum.tile([P, (e1 - e0) * C], F32, name="acc") for e0, e1 in BANK_EXPERTS]
+
+        def bank_of(e):
+            return [(bank, e0, e1) for bank, (e0, e1) in zip(banks, BANK_EXPERTS) if e0 <= e < e1][0]
 
         def multiply(e, a):
             cols = slice(e * C, (e + 1) * C)
-            weights = (
-                expert_words(open_parts, w_pass0, e).bitcast(FP8X4),
-                expert_words(open_parts, w_pass1, e).bitcast(FP4X4),
-                expert_words(close_parts, w_pass2, e).bitcast(FP4X4),
-            )[a]
+            bank, e0, e1 = bank_of(e)
             plane = e if a == 0 else E + 2 * e + a - 1
             nc.tensor.matmul_mx(
-                out=sums[e][:],
-                lhsT=weights,
+                out=bank[:, (e - e0) * C : (e - e0 + 1) * C],
+                lhsT=w_words[a][:, e, :].bitcast(FP4X4 if a else FP8X4),
                 lhsT_scale=w_scales[:, plane * N : (plane + 1) * N],
                 rhs=word_cols(a, e, e + 1).bitcast(FP8X4),
                 rhs_scale=(slot_scales[PLANE[0] : P, cols], slot_scales[:, cols], moved_scales[:, cols])[a],
-                start=(a == 0),
-                stop=(a == PASSES - 1),
+                start=(a == 0 and e == e0),
+                stop=(a == PASSES - 1 and e == e1 - 1),
             )
-
-        def open_group(e0):
-            for e in range(e0, e0 + GROUP):
-                sums[e] = psum.tile([P, C], F32, name="acc")
-                multiply(e, 0)
-                multiply(e, 1)
-
-        def gather_and_open(e0):
-            gather_words(1, e0, e0 + GROUP)
-            open_group(e0)
 
         def gather_and_close(e0, e1):
             gather_words(2, e0, e1)
             for e in range(e0, e1):
                 multiply(e, 2)
-                nc.scalar.activation(out=y[:, e * C : (e + 1) * C], in_=sums[e][:], func=GELU, bias=b_sb[:, e : e + 1])
+                bank, f0, f1 = bank_of(e)
+                if e == f1 - 1:
+                    for f in range(f0, f1):
+                        nc.scalar.activation(
+                            out=y[:, f * C : (f + 1) * C], in_=bank[:, (f - f0) * C : (f - f0 + 1) * C],
+                            func=GELU, bias=b_sb[:, f : f + 1],
+                        )
 
-        load_opening(2)
         gather_scales(0, 12)
-        load_closing(1)
-        load_opening(3)
-        load_closing(2)
-        open_group(0)
-        open_group(4)
-        gather_and_close(0, 8)
-        open_group(8)
+        for a in (0, 1):
+            for e in range(12):
+                multiply(e, a)
         gather_scales(12, E)
-        for r, pos in enumerate((pos1, pos2, pos3, pos4)):
-            nc.sync.dma_start(pos_sb[r][:], pos)
-        gather_and_open(12)
-        gather_and_close(8, 12)
-        gather_and_open(16)
-        gather_and_close(12, 16)
-        gather_and_close(16, 18)
-        gather_and_close(18, 19)
-        gather_and_close(19, E)
+        for r in range(4):
+            nc.sync.dma_start(out=moved_i32[r:P:32, :], in_=slot_scales[PLANE[2] + r : P : 32, :].bitcast(I32))
+        for e in range(12, E):
+            multiply(e, 0)
+        gather_words(1, 12, E)
+        for e in range(12, E):
+            multiply(e, 1)
+        gather_and_close(0, 8)
+        for e0, e1 in BANK_EXPERTS[2:]:
+            gather_and_close(e0, e1)
 
         token_parts = ((0, 2), (2, 4), (4, NB))
         prod = [keep.tile([P, T], F32, name=f"prod{r}") for r in range(TOP)]

@@ -14,6 +14,7 @@ FP4X4 = mybir.dt.float4_e2m1fn_x4
 MULT = mybir.AluOpType.mult
 ADD = mybir.AluOpType.add
 GELU = mybir.ActivationFunctionType.Gelu_apprx_tanh
+COPY = mybir.ActivationFunctionType.Copy
 
 P = 128
 K, T, E, C, N, TOP = 1536, 640, 20, 128, 128, 4
@@ -228,40 +229,79 @@ def tile_moe_tk_lin_gelu_kernel(
         for e0, e1 in BANK_EXPERTS[2:]:
             gather_and_close(e0, e1)
 
-        token_parts = ((0, 2), (2, 4), (4, NB))
-        prod = [keep.tile([P, T], F32, name=f"prod{r}") for r in range(TOP)]
+        part_a, part_b, part_c = (0, 2), (2, 4), (4, NB)
+        picked = keep.tile([P, TOP, T], F32, name="picked")
+        prod = keep.tile([P, TOP, T], F32, name="prod")
+        pairs = keep.tile([P, 2, P], F32, name="pairs")
         res = keep.tile([P, T], F32, name="res")
-        turned = [keep.tile([P, P], F32, name=f"turned{c}") for c in range(NB)]
-        three = [psum.tile([P, P], F32, name="acc") for c in range(NB)]
+
+        def cols_of(part):
+            return slice(part[0] * P, part[1] * P)
+
+        def token_list(r, part):
+            return pos_sb[r][:, part[0] * P // PER_COLUMN : part[1] * P // PER_COLUMN]
+
+        def pick(r, part):
+            nc.scalar.activation(out=picked[:, r, cols_of(part)], in_=y[:].indirect(token_list(r, part)), func=COPY)
+
+        def pick_weighted(r, part):
+            cols = cols_of(part)
+            nc.vector.tensor_tensor(prod[:, r, cols], y[:].indirect(token_list(r, part)), gate_sb[:, r, cols], MULT)
+
+        def weigh(r0, r1, part):
+            cols = cols_of(part)
+            nc.vector.tensor_tensor(prod[:, r0:r1, cols], picked[:, r0:r1, cols], gate_sb[:, r0:r1, cols], MULT)
+
+        sums = {part: psum.tile([P, 2 * P], F32, name="acc") for part in (part_a, part_b)}
         back = {}
 
-        def fetch(r, c0, c1):
-            cols = slice(c0 * P, c1 * P)
-            token_list = pos_sb[r][:, c0 * P // PER_COLUMN : c1 * P // PER_COLUMN]
-            nc.vector.tensor_tensor(prod[r][:, cols], y[:].indirect(token_list), gate_sb[:, r, cols], MULT)
-
-        def fetch_and_turn(r, c0, c1):
-            fetch(r, c0, c1)
-            for c in range(c0, c1):
+        def turn(r, part, first, last):
+            for c in range(*part):
                 nc.tensor.matmul(
-                    three[c][:], prod[r][:, c * P : (c + 1) * P], ident[:],
-                    start=(r == 0), stop=(r == TOP - 2), is_transpose=True,
+                    sums[part][:, (c - part[0]) * P : (c - part[0] + 1) * P], prod[:, r, c * P : (c + 1) * P], ident[:],
+                    start=(first and c == part[0]), stop=(last and c == part[1] - 1), is_transpose=True,
                 )
 
-        def turn_back(c0, c1):
-            back[c0] = psum.tile([P, (c1 - c0) * P], F32, name="acc")
-            for c in range(c0, c1):
-                nc.scalar.copy(out=turned[c][:], in_=three[c][:])
-                nc.tensor.transpose(back[c0][:, (c - c0) * P : (c - c0 + 1) * P], turned[c][:], ident[:])
+        def turn_back(part):
+            turned = keep.tile([P, 2 * P], F32, name=f"turned{part[0]}")
+            nc.scalar.copy(out=turned[:], in_=sums[part][:])
+            back[part] = psum.tile([P, 2 * P], F32, name="acc")
+            for j in range(2):
+                nc.tensor.transpose(back[part][:, j * P : (j + 1) * P], turned[:, j * P : (j + 1) * P], ident[:])
 
-        fetch_and_turn(0, 0, NB)
-        fetch_and_turn(1, 0, NB)
-        for c0, c1 in token_parts:
-            fetch_and_turn(2, c0, c1)
-            turn_back(c0, c1)
-        fetch(TOP - 1, 0, NB - 1)
-        fetch(TOP - 1, NB - 1, NB)
-        for c0, c1 in token_parts:
-            cols = slice(c0 * P, c1 * P)
-            nc.vector.tensor_tensor(res[:, cols], prod[TOP - 1][:, cols], back[c0][:], ADD)
+        def finish(part):
+            cols = cols_of(part)
+            nc.vector.tensor_tensor(res[:, cols], prod[:, TOP - 1, cols], back[part][:], ADD)
             nc.sync.dma_start(out=out[:, cols], in_=res[:, cols])
+
+        pick_weighted(0, part_a)
+        turn(0, part_a, True, False)
+        pick(1, part_a)
+        pick(2, part_a)
+        pick_weighted(0, part_b)
+        turn(0, part_b, True, False)
+        weigh(1, 2, part_a)
+        turn(1, part_a, False, False)
+        weigh(2, 3, part_a)
+        turn(2, part_a, False, True)
+        pick(1, part_b)
+        pick_weighted(2, part_b)
+        turn(2, part_b, False, False)
+        weigh(1, 2, part_b)
+        turn(1, part_b, False, True)
+        pick(3, part_a)
+        pick(0, part_c)
+        turn_back(part_a)
+        weigh(3, 4, part_a)
+        pick_weighted(3, part_b)
+        pick(1, part_c)
+        pick(2, part_c)
+        turn_back(part_b)
+        pick_weighted(3, part_c)
+        weigh(0, 3, part_c)
+        finish(part_a)
+        last = cols_of(part_c)
+        nc.vector.tensor_tensor(pairs[:], prod[:, 0:2, last], prod[:, 2:4, last], ADD)
+        finish(part_b)
+        nc.vector.tensor_tensor(res[:, last], pairs[:, 0, :], pairs[:, 1, :], ADD)
+        nc.sync.dma_start(out=out[:, last], in_=res[:, last])

@@ -229,10 +229,8 @@ def tile_moe_tk_lin_gelu_kernel(
         for e0, e1 in BANK_EXPERTS[2:]:
             gather_and_close(e0, e1)
 
-        part_a, part_b, part_c = (0, 2), (2, 4), (4, NB)
-        picked = keep.tile([P, TOP, T], F32, name="picked")
-        prod = keep.tile([P, TOP, T], F32, name="prod")
-        pairs = keep.tile([P, 2, P], F32, name="pairs")
+        part_a, part_b, part_c = (0, 2), (2, 3), (3, NB)
+        block_3, block_4 = (3, 4), (4, NB)
         res = keep.tile([P, T], F32, name="res")
 
         def cols_of(part):
@@ -241,67 +239,84 @@ def tile_moe_tk_lin_gelu_kernel(
         def token_list(r, part):
             return pos_sb[r][:, part[0] * P // PER_COLUMN : part[1] * P // PER_COLUMN]
 
-        def pick(r, part):
-            nc.scalar.activation(out=picked[:, r, cols_of(part)], in_=y[:].indirect(token_list(r, part)), func=COPY)
+        def pick(dst, r, part):
+            nc.scalar.activation(out=dst, in_=y[:].indirect(token_list(r, part)), func=COPY)
 
-        def pick_weighted(r, part):
-            cols = cols_of(part)
-            nc.vector.tensor_tensor(prod[:, r, cols], y[:].indirect(token_list(r, part)), gate_sb[:, r, cols], MULT)
+        def pick_weighted(dst, r, part):
+            nc.vector.tensor_tensor(dst, y[:].indirect(token_list(r, part)), gate_sb[:, r, cols_of(part)], MULT)
 
-        def weigh(r0, r1, part):
-            cols = cols_of(part)
-            nc.vector.tensor_tensor(prod[:, r0:r1, cols], picked[:, r0:r1, cols], gate_sb[:, r0:r1, cols], MULT)
+        def weigh(dst, src, r0, r1, part):
+            nc.vector.tensor_tensor(dst, src, gate_sb[:, r0:r1, cols_of(part)], MULT)
 
-        sums = {part: psum.tile([P, 2 * P], F32, name="acc") for part in (part_a, part_b)}
-        back = {}
-
-        def turn(r, part, first, last):
-            for c in range(*part):
+        def turn(bank, src, blocks, first, last):
+            for j in range(blocks):
                 nc.tensor.matmul(
-                    sums[part][:, (c - part[0]) * P : (c - part[0] + 1) * P], prod[:, r, c * P : (c + 1) * P], ident[:],
-                    start=(first and c == part[0]), stop=(last and c == part[1] - 1), is_transpose=True,
+                    bank[:, j * P : (j + 1) * P], src[:, j * P : (j + 1) * P], ident[:],
+                    start=(first and j == 0), stop=(last and j == blocks - 1), is_transpose=True,
                 )
 
-        def turn_back(part):
-            turned = keep.tile([P, 2 * P], F32, name=f"turned{part[0]}")
-            nc.scalar.copy(out=turned[:], in_=sums[part][:])
-            back[part] = psum.tile([P, 2 * P], F32, name="acc")
-            for j in range(2):
-                nc.tensor.transpose(back[part][:, j * P : (j + 1) * P], turned[:, j * P : (j + 1) * P], ident[:])
+        def turn_back(bank, part):
+            blocks = part[1] - part[0]
+            turned = keep.tile([P, blocks * P], F32, name=f"turned{part[0]}")
+            nc.scalar.copy(out=turned[:], in_=bank[:])
+            back = psum.tile([P, blocks * P], F32, name="acc")
+            for j in range(blocks):
+                nc.tensor.transpose(back[:, j * P : (j + 1) * P], turned[:, j * P : (j + 1) * P], ident[:])
+            return back
 
-        def finish(part):
-            cols = cols_of(part)
-            nc.vector.tensor_tensor(res[:, cols], prod[:, TOP - 1, cols], back[part][:], ADD)
-            nc.sync.dma_start(out=out[:, cols], in_=res[:, cols])
+        def store(part):
+            nc.sync.dma_start(out=out[:, cols_of(part)], in_=res[:, cols_of(part)])
 
-        pick_weighted(0, part_a)
-        turn(0, part_a, True, False)
-        pick(1, part_a)
-        pick(2, part_a)
-        pick_weighted(0, part_b)
-        turn(0, part_b, True, False)
-        weigh(1, 2, part_a)
-        turn(1, part_a, False, False)
-        weigh(2, 3, part_a)
-        turn(2, part_a, False, True)
-        pick(1, part_b)
-        pick_weighted(2, part_b)
-        turn(2, part_b, False, False)
-        weigh(1, 2, part_b)
-        turn(1, part_b, False, True)
-        pick(3, part_a)
-        pick(0, part_c)
-        turn_back(part_a)
-        weigh(3, 4, part_a)
-        pick_weighted(3, part_b)
-        pick(1, part_c)
-        pick(2, part_c)
-        turn_back(part_b)
-        pick_weighted(3, part_c)
-        weigh(0, 3, part_c)
-        finish(part_a)
-        last = cols_of(part_c)
-        nc.vector.tensor_tensor(pairs[:], prod[:, 0:2, last], prod[:, 2:4, last], ADD)
-        finish(part_b)
-        nc.vector.tensor_tensor(res[:, last], pairs[:, 0, :], pairs[:, 1, :], ADD)
-        nc.sync.dma_start(out=out[:, last], in_=res[:, last])
+        sum_a = psum.tile([P, 2 * P], F32, name="acc")
+        prod_a = keep.tile([P, 3, 2 * P], F32, name="prod_a")
+        prod_a3 = hold.tile([P, 1, 2 * P], F32, name="prod_a3", tag="hold5")
+        picked_a = keep.tile([P, 2, 2 * P], F32, name="picked_a")
+        for r in (0, 1):
+            pick_weighted(prod_a[:, r, :], r, part_a)
+            turn(sum_a, prod_a[:, r, :], 2, r == 0, False)
+            pick(picked_a[:, r, :], 2 + r, part_a)
+        weigh(prod_a[:, 2:3, :], picked_a[:, 0:1, :], 2, 3, part_a)
+        turn(sum_a, prod_a[:, 2, :], 2, False, False)
+        weigh(prod_a3[:], picked_a[:, 1:2, :], 3, 4, part_a)
+        turn(sum_a, prod_a3[:, 0, :], 2, False, True)
+
+        sum_b = psum.tile([P, P], F32, name="acc")
+        prod_b = keep.tile([P, 3, P], F32, name="prod_b")
+        prod_b3 = hold.tile([P, 1, P], F32, name="prod_b3", tag="hold6")
+        picked_b = keep.tile([P, 3, P], F32, name="picked_b")
+        for r in (1, 2, 3):
+            pick(picked_b[:, r - 1, :], r, part_b)
+        pick_weighted(prod_b[:, 0, :], 0, part_b)
+        weigh(prod_b[:, 1:3, :], picked_b[:, 0:2, :], 1, 3, part_b)
+        weigh(prod_b3[:], picked_b[:, 2:3, :], 3, 4, part_b)
+        for r in (0, 1, 2):
+            turn(sum_b, prod_b[:, r, :], 1, r == 0, False)
+        turn(sum_b, prod_b3[:, 0, :], 1, False, True)
+
+        prod_c = keep.tile([P, TOP, 2 * P], F32, name="prod_c")
+        picked_c0 = keep.tile([P, 1, 2 * P], F32, name="picked_c0")
+        sum_c = keep.tile([P, 2 * P], F32, name="sum_c")
+        pick(picked_c0[:, 0, :], 0, part_c)
+        back_a = turn_back(sum_a, part_a)
+        picked_c1 = hold.tile([P, 1, 2 * P], F32, name="picked_c1", tag="hold5")
+        pick(picked_c1[:, 0, :], 1, part_c)
+        back_b = turn_back(sum_b, part_b)
+        picked_c2 = hold.tile([P, 1, P], F32, name="picked_c2", tag="hold6")
+        pick(picked_c2[:, 0, :], 2, block_4)
+        nc.scalar.copy(out=res[:, cols_of(part_a)], in_=back_a[:])
+        store(part_a)
+        nc.scalar.copy(out=res[:, cols_of(part_b)], in_=back_b[:])
+        store(part_b)
+
+        pick_weighted(prod_c[:, 3, :], 3, part_c)
+        weigh(prod_c[:, 0:1, :], picked_c0[:], 0, 1, part_c)
+        pick_weighted(prod_c[:, 2, 0:P], 2, block_3)
+        nc.vector.tensor_tensor(sum_c[:], prod_c[:, 0, :], prod_c[:, 3, :], ADD)
+        weigh(prod_c[:, 1:2, :], picked_c1[:], 1, 2, part_c)
+        nc.vector.tensor_tensor(sum_c[:, 0:P], sum_c[:, 0:P], prod_c[:, 2, 0:P], ADD)
+        weigh(prod_c[:, 2:3, P:], picked_c2[:], 2, 3, block_4)
+        nc.vector.tensor_tensor(sum_c[:, P:], sum_c[:, P:], prod_c[:, 1, P:], ADD)
+        nc.vector.tensor_tensor(res[:, cols_of(block_3)], sum_c[:, 0:P], prod_c[:, 1, 0:P], ADD)
+        store(block_3)
+        nc.vector.tensor_tensor(res[:, cols_of(block_4)], sum_c[:, P:], prod_c[:, 2, P:], ADD)
+        store(block_4)

@@ -22,8 +22,11 @@ PASSES = 3
 S = E * C
 FLOPS = 2 * S * K * N
 
-BANKS = 8
+SUM_BANKS = 5
 BANK_EXPERTS = ((0, 4), (4, 8), (8, 12), (12, 15), (15, 17), (17, 18), (18, 19), (19, 20))
+EARLY = 17
+GATE_IN_PSUM = (((2, 0), (2, 1), (3, 0), (3, 1)), ((1, 2), (2, 2), (3, 2), (2, 4)), ((0, 3), (0, 4), (1, 3), (1, 4)))
+GATE_IN_SBUF = (((0, 0), (0, 1), (1, 0), (1, 1)), ((0, 2), (2, 3), (3, 3), (3, 4)))
 NB = T // P
 PER_COLUMN = 16
 TAIL = 896
@@ -40,7 +43,8 @@ def tile_moe_tk_lin_gelu_kernel(
         lists = ctx.enter_context(tc.tile_pool(name="lists", bufs=1))
         keep = ctx.enter_context(tc.tile_pool(name="keep", bufs=1))
         hold = ctx.enter_context(tc.tile_pool(name="hold", bufs=1))
-        psum = ctx.enter_context(tc.psum_pool(name="psum", bufs=BANKS))
+        psum = ctx.enter_context(tc.psum_pool(name="psum", bufs=SUM_BANKS))
+        gate_psum = ctx.enter_context(tc.psum_pool(name="gate_psum", bufs=1))
 
         offs_sb = lists.tile([P, S // PER_COLUMN], U16, name="offs_sb")
         pos_sb = [lists.tile([P, T // PER_COLUMN], U16, name=f"pos{r}_sb") for r in range(TOP)]
@@ -169,20 +173,34 @@ def tile_moe_tk_lin_gelu_kernel(
         turned_gate = psum.tile([P, P], F32, name="acc")
         nc.tensor.transpose(turned_gate[:], gate_rows[:], ident[:])
         nc.scalar.copy(out=gate_cols[:], in_=turned_gate[:, 0 : TOP * NB])
-        gate_sb = keep.tile([P, TOP, T], F32, name="gate_sb")
-        gate_flat = gate_sb[:].rearrange("p r t -> p (r t)")
-        for j0 in range(0, TOP * NB, 4):
-            spread = psum.tile([P, 4 * P], F32, name="acc")
-            for j in range(j0, j0 + 4):
-                nc.tensor.transpose(
-                    spread[:, (j - j0) * P : (j - j0 + 1) * P], gate_cols[:, j : j + 1].to_broadcast([P, P]), ident[:]
-                )
-            nc.scalar.copy(out=gate_flat[:, j0 * P : (j0 + 4) * P], in_=spread[:])
+        gate_of = {}
+
+        def spread(bank, entries):
+            for j, (r, c) in enumerate(entries):
+                column = gate_cols[:, r * NB + c : r * NB + c + 1]
+                nc.tensor.transpose(bank[:, j * P : (j + 1) * P], column.to_broadcast([P, P]), ident[:])
+
+        for i, entries in enumerate(GATE_IN_SBUF):
+            passing = psum.tile([P, 4 * P], F32, name="acc")
+            spread(passing, entries)
+            gate_sb = keep.tile([P, 4 * P], F32, name=f"gate_sb{i}")
+            nc.scalar.copy(out=gate_sb[:], in_=passing[:])
+            for j, entry in enumerate(entries):
+                gate_of[entry] = (gate_sb, j * P)
+        for i, entries in enumerate(GATE_IN_PSUM):
+            gate_bank = gate_psum.tile([P, 4 * P], F32, name=f"gate_bank{i}")
+            spread(gate_bank, entries)
+            for j, entry in enumerate(entries):
+                gate_of[entry] = (gate_bank, j * P)
+
+        def gate_run(r, c, blocks):
+            tile_of_gate, first = gate_of[(r, c)]
+            return tile_of_gate[:, first : first + blocks * P]
 
         y = keep.tile([P, S], F32, name="y")
         moved_scales = moved_i32[:].bitcast(U8)
         w_scales = w_scales_i32[:].bitcast(U8)
-        banks = [psum.tile([P, (e1 - e0) * C], F32, name="acc") for e0, e1 in BANK_EXPERTS]
+        banks = [psum.tile([P, (e1 - e0) * C], F32, name="acc") for e0, e1 in BANK_EXPERTS[:SUM_BANKS]]
 
         def bank_of(e):
             return [(bank, e0, e1) for bank, (e0, e1) in zip(banks, BANK_EXPERTS) if e0 <= e < e1][0]
@@ -220,13 +238,25 @@ def tile_moe_tk_lin_gelu_kernel(
         gather_scales(12, E)
         for r in range(4):
             nc.sync.dma_start(out=moved_i32[r:P:32, :], in_=slot_scales[PLANE[2] + r : P : 32, :].bitcast(I32))
-        for e in range(12, E):
+        for e in range(12, EARLY):
             multiply(e, 0)
         gather_words(1, 12, E)
-        for e in range(12, E):
+        for e in range(12, EARLY):
             multiply(e, 1)
+
+        def open_late(e):
+            banks.append(psum.tile([P, C], F32, name="acc"))
+            multiply(e, 0)
+            multiply(e, 1)
+
         gather_and_close(0, 8)
-        for e0, e1 in BANK_EXPERTS[2:]:
+        gather_and_close(8, 12)
+        open_late(EARLY)
+        gather_and_close(12, 15)
+        open_late(EARLY + 1)
+        gather_and_close(15, 17)
+        open_late(EARLY + 2)
+        for e0, e1 in BANK_EXPERTS[SUM_BANKS:]:
             gather_and_close(e0, e1)
 
         part_a, part_b, part_c = (0, 2), (2, 3), (3, NB)
@@ -243,10 +273,11 @@ def tile_moe_tk_lin_gelu_kernel(
             nc.scalar.activation(out=dst, in_=y[:].indirect(token_list(r, part)), func=COPY)
 
         def pick_weighted(dst, r, part):
-            nc.vector.tensor_tensor(dst, y[:].indirect(token_list(r, part)), gate_sb[:, r, cols_of(part)], MULT)
+            nc.vector.tensor_tensor(dst, y[:].indirect(token_list(r, part)), gate_run(r, part[0], part[1] - part[0]), MULT)
 
         def weigh(dst, src, r0, r1, part):
-            nc.vector.tensor_tensor(dst, src, gate_sb[:, r0:r1, cols_of(part)], MULT)
+            weights = gate_run(r0, part[0], (r1 - r0) * (part[1] - part[0]))
+            nc.vector.tensor_tensor(dst, src, weights.rearrange("p (r t) -> p r t", r=r1 - r0), MULT)
 
         def turn(bank, src, blocks, first, last):
             for j in range(blocks):

from contextlib import ExitStack

import concourse.mybir as mybir
from concourse.masks import make_identity

F32 = mybir.dt.float32
BF16 = mybir.dt.bfloat16
I32 = mybir.dt.int32
U32 = mybir.dt.uint32
U16 = mybir.dt.uint16
U8 = mybir.dt.uint8
FP8X4 = mybir.dt.float8_e4m3fn_x4
FP4X4 = mybir.dt.float4_e2m1fn_x4
MULT = mybir.AluOpType.mult
ADD = mybir.AluOpType.add
GELU = mybir.ActivationFunctionType.Gelu_apprx_tanh
COPY = mybir.ActivationFunctionType.Copy

P = 128
K, T, E, C, N, TOP = 1536, 640, 20, 128, 128, 4
PASSES = 3
S = E * C
FLOPS = 2 * S * K * N

SUM_BANKS = 5
BANK_EXPERTS = ((0, 4), (4, 8), (8, 12), (12, 15), (15, 17), (17, 18), (18, 19), (19, 20))
EARLY = 17
GATE_IN_PSUM = (((2, 0), (2, 1), (3, 0), (3, 1)), ((1, 2), (2, 2), (3, 2), (2, 4)), ((0, 3), (0, 4), (1, 3), (1, 4)))
GATE_IN_SBUF = (((0, 0), (0, 1), (1, 0), (1, 1)), ((0, 2), (2, 3), (3, 3), (3, 4)))
NB = T // P
PER_COLUMN = 16
TAIL = 896
WINDOW_LEAST = T + 64
WINDOW_BYTES = 2048
PLANE = (4, 0, 8)


def tile_moe_tk_lin_gelu_kernel(
    tc, xT, w8_words, w8_scales, w4_words, w4_scales, b, gate, offs, pos1, pos2, pos3, pos4, out
):
    nc = tc.nc
    with ExitStack() as ctx:
        lists = ctx.enter_context(tc.tile_pool(name="lists", bufs=1))
        keep = ctx.enter_context(tc.tile_pool(name="keep", bufs=1))
        hold = ctx.enter_context(tc.tile_pool(name="hold", bufs=1))
        psum = ctx.enter_context(tc.psum_pool(name="psum", bufs=SUM_BANKS))
        gate_psum = ctx.enter_context(tc.psum_pool(name="gate_psum", bufs=1))

        offs_sb = lists.tile([P, S // PER_COLUMN], U16, name="offs_sb")
        pos_sb = [lists.tile([P, T // PER_COLUMN], U16, name=f"pos{r}_sb") for r in range(TOP)]

        def x_rows(a):
            return xT[512 * a : 512 * (a + 1), :].rearrange("(p j) t -> p j t", j=4)

        x0a = keep.tile([P, 4, 256], F32, name="x0a")
        x0b = keep.tile([P, 4, 256], F32, name="x0b")
        x0c = keep.tile([P, 4, 128], F32, name="x0c")
        x1a = hold.tile([P, 4, T // 2], F32, name="x1a", tag="hold4", align_bytes=64)
        x1b = hold.tile([P, 4, T // 2], F32, name="x1b", tag="hold1", align_bytes=64)
        x2 = hold.tile([P, 4, T], F32, name="x2", tag="hold2", align_bytes=64)
        nc.sync.dma_start(out=x0a[:], in_=x_rows(0)[:, :, 0:256])
        nc.sync.dma_start(out=x0b[:], in_=x_rows(0)[:, :, 256:512])
        nc.sync.dma_start(out=x0c[:], in_=x_rows(0)[:, :, 512:T])
        nc.sync.dma_start(offs_sb[:], offs)
        nc.sync.dma_start(out=x1a[:], in_=x_rows(1)[:, :, 0 : T // 2])
        nc.sync.dma_start(out=x1b[:], in_=x_rows(1)[:, :, T // 2 : T])
        stage = keep.tile([P, PASSES * E, N // 4], I32, name="stage")
        nc.sync.dma_start(out=stage[0:P:8, 0:E, :], in_=w8_scales.bitcast(I32).rearrange("e a q n -> q (e a) n"))
        nc.sync.dma_start(out=stage[0:P:8, E:, :], in_=w4_scales.bitcast(I32).rearrange("e a q n -> q (e a) n"))
        nc.sync.dma_start(out=x2[:], in_=x_rows(2))

        warm_in = keep.tile([P, 8], F32, name="tiny")
        warm_out = keep.tile([P, 8], F32, name="tiny2")
        nc.gpsimd.memset(warm_in[:], 0.0)
        nc.scalar.activation(out=warm_out[:], in_=warm_in[:], func=GELU)

        codes_all = keep.tile([P, PASSES * T + TAIL], I32, name="codes_all", align_bytes=64)
        codes = [codes_all[:, (PASSES - 1 - a) * T :] for a in range(PASSES)]
        token_scales_i32 = keep.tile([P, WINDOW_BYTES // 4], I32, name="bytes_i32", align_bytes=64)
        token_scales = token_scales_i32[:].bitcast(U8)
        nc.vector.memset(token_scales_i32[:], 0)
        nc.vector.memset(codes[0][:, T:], 0)
        w_scales_i32 = keep.tile([P, PASSES * E * N // 4], I32, name="w_s", align_bytes=64)
        moved_i32 = keep.tile([P, S // 4], I32, name="g_moved", align_bytes=64)
        nc.vector.memset(w_scales_i32[:], 0)
        nc.vector.memset(moved_i32[:], 0)
        ident = keep.tile([P, P], F32, name="ident")
        make_identity(nc, ident[:])

        gate_rows = keep.tile([P, P], F32, name="gate_rows")
        nc.vector.memset(gate_rows[:], 0.0)
        nc.sync.dma_start(out=gate_rows[0 : TOP * NB, :], in_=gate[:, 0, :].rearrange("r (c p) -> r c p", p=P))
        b_sb = keep.tile([P, E], F32, name="b_sb")
        nc.sync.dma_start(out=b_sb[:], in_=b)

        w_words = [keep.tile([P, E, N // (2 if a else 1)], I32, name=f"w_pass{a}", align_bytes=64) for a in range(PASSES)]
        for r in range(4):
            nc.sync.dma_start(out=w_scales_i32[r:P:32, :], in_=stage[8 * r : P : 32, :, :].rearrange("p g n -> p (g n)"))
        nc.sync.dma_start(out=w_words[0][:], in_=w8_words.rearrange("e a p n r -> p (e a) (n r)").bitcast(I32))
        for a in (1, 2):
            nc.sync.dma_start(out=w_words[a][:], in_=w4_words[:, a - 1].rearrange("e p n -> p e n").bitcast(I32))
        for r, pos in enumerate((pos1, pos2, pos3, pos4)):
            nc.sync.dma_start(pos_sb[r][:], pos)

        xb = [keep.tile([P, T, 4], BF16, name=f"xb{a}", align_bytes=64) for a in range(2)]
        xb.append(hold.tile([P, T, 4], BF16, name="xb2", tag="hold3", align_bytes=64))

        def round_tokens(copy, a, src, t0, t1, src_t0):
            copy(
                out=xb[a][:, t0:t1, :].rearrange("p (c i) j -> p c j i", i=4),
                in_=src[:, :, t0 - src_t0 : t1 - src_t0].rearrange("p j (c i) -> p c j i", i=4),
            )

        def quantise(a, t0, t1):
            nc.vector.quantize_mx(
                out=codes[a][:, t0:t1].bitcast(FP8X4),
                scales=token_scales[PLANE[a] : P, t0:t1],
                in_=xb[a][:, t0:t1, :].rearrange("p n j -> p (n j)"),
            )

        slot_words = {a: [] for a in range(PASSES)}
        slot_scales = keep.tile([P, S], U8, name="g_bytes", align_bytes=64)

        def word_tile(a, e0, e1, pool, tag):
            tile_words = pool.tile([P, (e1 - e0) * C], U32, name=f"words{a}_{e0 * C}", tag=tag, align_bytes=64)
            slot_words[a].append((e0, e1, tile_words))

        def word_cols(a, e0, e1):
            return [t[:, (e0 - f0) * C : (e1 - f0) * C] for f0, f1, t in slot_words[a] if f0 <= e0 and e1 <= f1][0]

        def slot_list(e0, e1):
            return offs_sb[:, e0 * C // PER_COLUMN : e1 * C // PER_COLUMN]

        def gather_words(a, e0, e1):
            count = (e1 - e0) * C
            window = max(WINDOW_LEAST, count * 3 // 2 if a else count * 4 // 3)
            nc.vector.tensor_copy(out=word_cols(a, e0, e1), in_=codes[a][:, 0:window].bitcast(U32).indirect(slot_list(e0, e1)))

        def gather_scales(e0, e1):
            nc.vector.tensor_copy(out=slot_scales[:, e0 * C : e1 * C], in_=token_scales.indirect(slot_list(e0, e1)))

        round_tokens(nc.vector.tensor_copy, 0, x0a, 0, 128, 0)
        round_tokens(nc.scalar.copy, 0, x0a, 128, 256, 0)
        quantise(0, 0, 256)
        round_tokens(nc.vector.tensor_copy, 0, x0b, 256, 416, 256)
        round_tokens(nc.scalar.copy, 0, x0b, 416, 512, 256)
        quantise(0, 256, 512)
        round_tokens(nc.vector.tensor_copy, 0, x0c, 512, 608, 512)
        round_tokens(nc.scalar.copy, 0, x0c, 608, T, 512)
        quantise(0, 512, T)
        round_tokens(nc.scalar.copy, 1, x1a, 0, T // 2, 0)
        round_tokens(nc.scalar.copy, 1, x1b, T // 2, T, T // 2)
        round_tokens(nc.scalar.copy, 2, x2, 0, 512, 0)
        round_tokens(nc.scalar.copy, 2, x2, 512, T, 0)

        word_tile(0, 0, 18, keep, "w0a")
        word_tile(1, 0, 10, keep, "w1a")
        word_tile(2, 0, E, keep, "w2")
        gather_words(0, 0, 9)
        gather_words(0, 9, 18)
        quantise(1, 0, 512)
        quantise(1, 512, T)
        word_tile(0, 18, E, hold, "hold1")
        gather_words(0, 18, E)
        gather_words(1, 0, 10)
        quantise(2, 0, 512)
        quantise(2, 512, T)
        word_tile(1, 10, 12, hold, "hold2")
        gather_words(1, 10, 12)
        word_tile(1, 12, E, hold, "hold3")

        gate_cols = hold.tile([P, TOP * NB], F32, name="gate_cols", tag="hold4", align_bytes=64)
        turned_gate = psum.tile([P, P], F32, name="acc")
        nc.tensor.transpose(turned_gate[:], gate_rows[:], ident[:])
        nc.scalar.copy(out=gate_cols[:], in_=turned_gate[:, 0 : TOP * NB])
        gate_of = {}

        def spread(bank, entries):
            for j, (r, c) in enumerate(entries):
                column = gate_cols[:, r * NB + c : r * NB + c + 1]
                nc.tensor.transpose(bank[:, j * P : (j + 1) * P], column.to_broadcast([P, P]), ident[:])

        for i, entries in enumerate(GATE_IN_SBUF):
            passing = psum.tile([P, 4 * P], F32, name="acc")
            spread(passing, entries)
            gate_sb = keep.tile([P, 4 * P], F32, name=f"gate_sb{i}")
            nc.scalar.copy(out=gate_sb[:], in_=passing[:])
            for j, entry in enumerate(entries):
                gate_of[entry] = (gate_sb, j * P)
        for i, entries in enumerate(GATE_IN_PSUM):
            gate_bank = gate_psum.tile([P, 4 * P], F32, name=f"gate_bank{i}")
            spread(gate_bank, entries)
            for j, entry in enumerate(entries):
                gate_of[entry] = (gate_bank, j * P)

        def gate_run(r, c, blocks):
            tile_of_gate, first = gate_of[(r, c)]
            return tile_of_gate[:, first : first + blocks * P]

        y = keep.tile([P, S], F32, name="y")
        moved_scales = moved_i32[:].bitcast(U8)
        w_scales = w_scales_i32[:].bitcast(U8)
        banks = [psum.tile([P, (e1 - e0) * C], F32, name="acc") for e0, e1 in BANK_EXPERTS[:SUM_BANKS]]

        def bank_of(e):
            return [(bank, e0, e1) for bank, (e0, e1) in zip(banks, BANK_EXPERTS) if e0 <= e < e1][0]

        def multiply(e, a):
            cols = slice(e * C, (e + 1) * C)
            bank, e0, e1 = bank_of(e)
            plane = e if a == 0 else E + 2 * e + a - 1
            nc.tensor.matmul_mx(
                out=bank[:, (e - e0) * C : (e - e0 + 1) * C],
                lhsT=w_words[a][:, e, :].bitcast(FP4X4 if a else FP8X4),
                lhsT_scale=w_scales[:, plane * N : (plane + 1) * N],
                rhs=word_cols(a, e, e + 1).bitcast(FP8X4),
                rhs_scale=(slot_scales[PLANE[0] : P, cols], slot_scales[:, cols], moved_scales[:, cols])[a],
                start=(a == 0 and e == e0),
                stop=(a == PASSES - 1 and e == e1 - 1),
            )

        def gather_and_close(e0, e1):
            gather_words(2, e0, e1)
            for e in range(e0, e1):
                multiply(e, 2)
                bank, f0, f1 = bank_of(e)
                if e == f1 - 1:
                    for f in range(f0, f1):
                        nc.scalar.activation(
                            out=y[:, f * C : (f + 1) * C], in_=bank[:, (f - f0) * C : (f - f0 + 1) * C],
                            func=GELU, bias=b_sb[:, f : f + 1],
                        )

        gather_scales(0, 12)
        for a in (0, 1):
            for e in range(12):
                multiply(e, a)
        gather_scales(12, E)
        for r in range(4):
            nc.sync.dma_start(out=moved_i32[r:P:32, :], in_=slot_scales[PLANE[2] + r : P : 32, :].bitcast(I32))
        for e in range(12, EARLY):
            multiply(e, 0)
        gather_words(1, 12, E)
        for e in range(12, EARLY):
            multiply(e, 1)

        def open_late(e):
            banks.append(psum.tile([P, C], F32, name="acc"))
            multiply(e, 0)
            multiply(e, 1)

        gather_and_close(0, 8)
        gather_and_close(8, 12)
        open_late(EARLY)
        gather_and_close(12, 15)
        open_late(EARLY + 1)
        gather_and_close(15, 17)
        open_late(EARLY + 2)
        for e0, e1 in BANK_EXPERTS[SUM_BANKS:]:
            gather_and_close(e0, e1)

        part_a, part_b, part_c = (0, 2), (2, 3), (3, NB)
        block_3, block_4 = (3, 4), (4, NB)
        res = keep.tile([P, T], F32, name="res")

        def cols_of(part):
            return slice(part[0] * P, part[1] * P)

        def token_list(r, part):
            return pos_sb[r][:, part[0] * P // PER_COLUMN : part[1] * P // PER_COLUMN]

        def pick(dst, r, part):
            nc.scalar.activation(out=dst, in_=y[:].indirect(token_list(r, part)), func=COPY)

        def pick_weighted(dst, r, part):
            nc.vector.tensor_tensor(dst, y[:].indirect(token_list(r, part)), gate_run(r, part[0], part[1] - part[0]), MULT)

        def weigh(dst, src, r0, r1, part):
            weights = gate_run(r0, part[0], (r1 - r0) * (part[1] - part[0]))
            nc.vector.tensor_tensor(dst, src, weights.rearrange("p (r t) -> p r t", r=r1 - r0), MULT)

        def turn(bank, src, blocks, first, last):
            for j in range(blocks):
                nc.tensor.matmul(
                    bank[:, j * P : (j + 1) * P], src[:, j * P : (j + 1) * P], ident[:],
                    start=(first and j == 0), stop=(last and j == blocks - 1), is_transpose=True,
                )

        def turn_back(bank, part):
            blocks = part[1] - part[0]
            turned = keep.tile([P, blocks * P], F32, name=f"turned{part[0]}")
            nc.scalar.copy(out=turned[:], in_=bank[:])
            back = psum.tile([P, blocks * P], F32, name="acc")
            for j in range(blocks):
                nc.tensor.transpose(back[:, j * P : (j + 1) * P], turned[:, j * P : (j + 1) * P], ident[:])
            return back

        def store(part):
            nc.sync.dma_start(out=out[:, cols_of(part)], in_=res[:, cols_of(part)])

        sum_a = psum.tile([P, 2 * P], F32, name="acc")
        prod_a = keep.tile([P, 3, 2 * P], F32, name="prod_a")
        prod_a3 = hold.tile([P, 1, 2 * P], F32, name="prod_a3", tag="hold5")
        picked_a = keep.tile([P, 2, 2 * P], F32, name="picked_a")
        for r in (0, 1):
            pick_weighted(prod_a[:, r, :], r, part_a)
            turn(sum_a, prod_a[:, r, :], 2, r == 0, False)
            pick(picked_a[:, r, :], 2 + r, part_a)
        weigh(prod_a[:, 2:3, :], picked_a[:, 0:1, :], 2, 3, part_a)
        turn(sum_a, prod_a[:, 2, :], 2, False, False)
        weigh(prod_a3[:], picked_a[:, 1:2, :], 3, 4, part_a)
        turn(sum_a, prod_a3[:, 0, :], 2, False, True)

        sum_b = psum.tile([P, P], F32, name="acc")
        prod_b = keep.tile([P, 3, P], F32, name="prod_b")
        prod_b3 = hold.tile([P, 1, P], F32, name="prod_b3", tag="hold6")
        picked_b = keep.tile([P, 3, P], F32, name="picked_b")
        for r in (1, 2, 3):
            pick(picked_b[:, r - 1, :], r, part_b)
        pick_weighted(prod_b[:, 0, :], 0, part_b)
        weigh(prod_b[:, 1:3, :], picked_b[:, 0:2, :], 1, 3, part_b)
        weigh(prod_b3[:], picked_b[:, 2:3, :], 3, 4, part_b)
        for r in (0, 1, 2):
            turn(sum_b, prod_b[:, r, :], 1, r == 0, False)
        turn(sum_b, prod_b3[:, 0, :], 1, False, True)

        prod_c = keep.tile([P, TOP, 2 * P], F32, name="prod_c")
        picked_c0 = keep.tile([P, 1, 2 * P], F32, name="picked_c0")
        sum_c = keep.tile([P, 2 * P], F32, name="sum_c")
        pick(picked_c0[:, 0, :], 0, part_c)
        back_a = turn_back(sum_a, part_a)
        picked_c1 = hold.tile([P, 1, 2 * P], F32, name="picked_c1", tag="hold5")
        pick(picked_c1[:, 0, :], 1, part_c)
        back_b = turn_back(sum_b, part_b)
        picked_c2 = hold.tile([P, 1, P], F32, name="picked_c2", tag="hold6")
        pick(picked_c2[:, 0, :], 2, block_4)
        nc.scalar.copy(out=res[:, cols_of(part_a)], in_=back_a[:])
        store(part_a)
        nc.scalar.copy(out=res[:, cols_of(part_b)], in_=back_b[:])
        store(part_b)

        pick_weighted(prod_c[:, 3, :], 3, part_c)
        weigh(prod_c[:, 0:1, :], picked_c0[:], 0, 1, part_c)
        pick_weighted(prod_c[:, 2, 0:P], 2, block_3)
        nc.vector.tensor_tensor(sum_c[:], prod_c[:, 0, :], prod_c[:, 3, :], ADD)
        weigh(prod_c[:, 1:2, :], picked_c1[:], 1, 2, part_c)
        nc.vector.tensor_tensor(sum_c[:, 0:P], sum_c[:, 0:P], prod_c[:, 2, 0:P], ADD)
        weigh(prod_c[:, 2:3, P:], picked_c2[:], 2, 3, block_4)
        nc.vector.tensor_tensor(sum_c[:, P:], sum_c[:, P:], prod_c[:, 1, P:], ADD)
        nc.vector.tensor_tensor(res[:, cols_of(block_3)], sum_c[:, 0:P], prod_c[:, 1, 0:P], ADD)
        store(block_3)
        nc.vector.tensor_tensor(res[:, cols_of(block_4)], sum_c[:, P:], prod_c[:, 2, P:], ADD)
        store(block_4)
